import numpy as np
import ml_dtypes


def mxq(x, axis, fmt="e4m3"):
    dtype, down = {"e4m3": (ml_dtypes.float8_e4m3fn, 7), "e5m2": (ml_dtypes.float8_e5m2, 14)}[fmt]
    v = np.moveaxis(np.asarray(x, np.float32).astype(ml_dtypes.bfloat16).astype(np.float64), axis, -1)
    blocks = v.reshape(v.shape[:-1] + (-1, 32))
    amax = np.abs(blocks).max(-1, keepdims=True)
    byte = np.maximum(np.where(amax > 0, np.frexp(amax)[1] - 1 + 127, 0) - down, 1)
    scale = np.exp2(byte - 127.0)
    codes = (blocks / scale).astype(np.float32).astype(dtype).astype(np.float64)
    return np.moveaxis((codes * scale).reshape(v.shape), -1, axis)


WIDE = False


def mx_kscale(k):
    if not WIDE:
        return np.ones(k)
    levels = np.array([10, -10, 5, -5, 0])
    if k % 512:
        return np.exp2(np.random.permutation(np.resize(levels, k // 32))).repeat(32)
    a = np.empty((k // 512, 16))
    for p in range(k // 512):
        a[p, :8] = np.random.permutation(np.resize(levels, 8))
        for g in range(8):
            far = levels[np.abs(levels - a[p, g]) >= 10]
            a[p, g + 8] = far[np.random.randint(len(far))]
    return np.exp2(a.ravel()).repeat(32)


def f64(x):
    return np.asarray(x).astype(np.float64)


def striped(idx):
    return np.tile(idx.reshape(-1, 16).T, (8, 1)).astype(np.uint16)


def unstriped(offs):
    return offs[:16].T.reshape(-1).astype(np.int64)


E2M1 = np.array([0.0, 0.5, 1.0, 1.5, 2.0, 3.0, 4.0, 6.0, -0.0, -0.5, -1.0, -1.5, -2.0, -3.0, -4.0, -6.0])


def pack_weight(w, fmt):
    k, n = w.shape
    w = f64(np.asarray(w, np.float32).astype(ml_dtypes.bfloat16)).reshape(k // 32, 32, n)
    amax = np.abs(w).max(1)
    if fmt == "e4m3":
        byte = np.frexp(amax)[1] - 1 + 127 - 7
    else:
        mant, ex = np.frexp(amax / 6.0)
        byte = np.where(mant > 0.5, ex, ex - 1) + 127
    byte = np.clip(np.where(amax > 0, byte, 1), 1, 254)
    scaled = (w * np.exp2(127.0 - byte)[:, None, :]).reshape(k, n).astype(np.float32)
    by_word = np.ascontiguousarray(scaled.reshape(k // 512, 128, 4, n).transpose(0, 1, 3, 2))
    if fmt == "e4m3":
        words = by_word.astype(ml_dtypes.float8_e4m3fn).view(np.uint8)
    else:
        c = by_word.astype(ml_dtypes.float4_e2m1fn).view(np.uint8) & 0xF
        words = (c[..., 0::2] | (c[..., 1::2] << 4)).reshape(k // 512, 128, 2 * n)
    return np.ascontiguousarray(words), np.ascontiguousarray(byte.astype(np.uint8).reshape(k // 512, 16, n))


def unpack_weight(words, scales, fmt):
    g, _, n = scales.shape
    words = np.ascontiguousarray(words).reshape(g, 128, n, -1)
    if fmt == "e4m3":
        vals = words.view(ml_dtypes.float8_e4m3fn).astype(np.float64)
    else:
        nib = np.empty((g, 128, n, 4), np.uint8)
        nib[..., 0::2] = words & 0xF
        nib[..., 1::2] = words >> 4
        vals = E2M1[nib]
    vals = vals * np.repeat(np.exp2(scales.astype(np.float64) - 127.0), 8, axis=1)[..., None]
    return vals.transpose(0, 1, 3, 2).reshape(g * 512, n)


def gelu(v):
    return 0.5 * v * (1.0 + np.tanh(np.sqrt(2.0 / np.pi) * (v + 0.044715 * v**3)))


K, H, N, T, S, T2, P = 1536, 1024, 768, 2048, 1024, 2048, 512


def setup_inputs():
    n = np.random.standard_normal
    s = mx_kscale(K)[:, None]
    u = mx_kscale(H)[:, None]
    tab_words, tab_scales = pack_weight(n((K, T)) * s, "e4m3")
    w4_words, w4_scales = pack_weight(n((H, N)) / np.sqrt(H) / u, "e2m1")
    sign = np.where(n(H) > 0, 1.0, -1.0)
    return {
        "tab_words": tab_words, "tab_scales": tab_scales,
        "offs": striped(np.random.permutation(T)[:S]),
        "offs2": striped(np.random.permutation(T2)[:S]),
        "offs3": striped(np.random.permutation(T2)[:P]),
        "w1": (0.7 * n((K, H)) / np.sqrt(K) / s).astype(np.float32),
        "room": np.random.uniform(0.3, 1.7, (H, S)).astype(np.float32),
        "wgs": np.exp(0.3 * n((128, S))).astype(np.float32),
        "page0": (0.8 * n((H, T2))).astype(np.float32),
        "sharp": np.random.uniform(1, 3, H).astype(np.float32),
        "share": np.random.uniform(0.1, 0.5, H).astype(np.float32),
        "least": np.random.uniform(0.05, 0.25, H).astype(np.float32),
        "gain": (sign * np.random.uniform(1.5, 4.5, H) * u[:, 0]).astype(np.float32),
        "w4_words": w4_words, "w4_scales": w4_scales,
        "w3": (n((H, N)) / np.sqrt(H) / u).astype(np.float32),
        "bal": n((N, P)).astype(np.float32),
    }


def reference(tab_words, tab_scales, offs, offs2, offs3, w1, room, wgs, page0,
              sharp, share, least, gain, w4_words, w4_scales, w3, bal):
    v = unpack_weight(tab_words, tab_scales, "e4m3")[:, unstriped(offs)]
    h = f64(room) * (mxq(f64(w1), 0, "e4m3").T @ v)
    page = f64(page0).copy()
    page[:, unstriped(offs2)] = np.tile(f64(wgs), (H // 128, 1)) * h
    top = page.max(axis=1)
    x = 1.0 / (1.0 + np.exp(-f64(sharp)[:, None] * (page[:, unstriped(offs3)] - f64(share)[:, None] * top[:, None])))
    y = f64(gain)[:, None] * np.maximum(x, f64(least)[:, None])
    yq = mxq(y, 0, "e4m3")
    w4 = unpack_weight(w4_words, w4_scales, "e2m1")
    local = f64(bal) * (w4.T @ yq)
    return local + (mxq(f64(w3), 0, "e4m3").T @ yq)

@@ -1,0 +1,352 @@
+from contextlib import ExitStack
+
+import concourse.mybir as mybir
+
+K, H, N, T, S, T2, M = 1536, 1024, 768, 2048, 1024, 2048, 512
+FLOPS = 2 * K * H * S + 2 * 2 * H * N * M
+
+F32 = mybir.dt.float32
+BF16 = mybir.dt.bfloat16
+I32 = mybir.dt.int32
+U32 = mybir.dt.uint32
+U16 = mybir.dt.uint16
+U8 = mybir.dt.uint8
+FP8X4 = mybir.dt.float8_e4m3fn_x4
+FP4X4 = mybir.dt.float4_e2m1fn_x4
+ACT = mybir.ActivationFunctionType
+ALU = mybir.AluOpType
+AXIS = mybir.AxisListType
+
+P = 128
+PACK = 4
+PASS = P * PACK
+BANK = 512
+KP = K // PASS
+HP = H // PASS
+TILES = HP * PACK
+NT = N // P
+W3_PIECE = 384
+
+
+def tile_list_box_placement_balance_kernel(
+    tc, tab_words, tab_scales, offs, offs2, offs3, w1, room, wgs, page0,
+    sharp, share, least, gain, w4_words, w4_scales, w3, bal, out,
+):
+    nc = tc.nc
+    with ExitStack() as ctx:
+        lists = ctx.enter_context(tc.tile_pool(name="lists", bufs=1))
+        keep = ctx.enter_context(tc.tile_pool(name="keep", bufs=1))
+        stage = ctx.enter_context(tc.tile_pool(name="stage", bufs=3))
+        pages = ctx.enter_context(tc.tile_pool(name="pages", bufs=5))
+        work = ctx.enter_context(tc.tile_pool(name="work", bufs=2))
+        late = ctx.enter_context(tc.tile_pool(name="late", bufs=1))
+        scores = ctx.enter_context(tc.tile_pool(name="scores", bufs=1))
+        psum = ctx.enter_context(tc.psum_pool(name="psum", bufs=1))
+
+        idx = lists.tile([P, S // 16], U16, name="idx")
+        idx2 = lists.tile([P, S // 16], U16, name="idx2")
+        idx3 = lists.tile([P, M // 16], U16, name="idx3")
+
+        tab_w = [keep.tile([P, T], I32, name="tab_w%d" % a) for a in range(KP)]
+        tab_s = keep.tile([P, T], U8, name="tab_s")
+        v_w = [[keep.tile([P, BANK], U32, name="v_w%d_%d" % (a, c), align_bytes=64) for c in range(2)] for a in range(KP)]
+        v_s = keep.tile([P, S], U8, name="v_s", align_bytes=64)
+        w1_c = {}
+        w1_s = {}
+        w3_c = {}
+        w3_s = {}
+        y_c = {}
+        y_s = {}
+        y_bf = {}
+        room_t = {}
+        page_t = {}
+        h_t = {}
+        wgs_t = [keep.tile([P, S], F32, name="wgs%d" % i) for i in range(PACK)]
+        halves = [slice(BANK * c, BANK * (c + 1)) for c in range(2)]
+        whole = slice(0, S)
+        acc1 = {}
+        acc2 = {}
+        bal_t = {}
+        top = {}
+        bias = keep.tile([P, TILES], F32, name="bias")
+
+        def rows(ap, t):
+            b, i = divmod(t, PACK)
+            return ap.rearrange("(b p i) c -> b i p c", b=HP, i=PACK)[b, i]
+
+        def load_tab(a):
+            nc.sync.dma_start(out=tab_w[a][:], in_=tab_words[a].rearrange("p t i -> p (t i)").bitcast(I32))
+
+        def gather_words(a, c):
+            nc.vector.tensor_copy(out=v_w[a][c][:], in_=tab_w[a][:].bitcast(U32).indirect(idx[:, 32 * c : 32 * c + 32]))
+
+        def load_w1(a, b):
+            raw = stage.tile([P, PACK, PASS], F32, name="raw", tag="raw")
+            src = w1[PASS * a : PASS * (a + 1), PASS * b : PASS * (b + 1)]
+            nc.sync.dma_start(out=raw[:], in_=src.rearrange("(p j) c -> p j c", j=PACK))
+            return raw
+
+        def on_scores(t, at, shape, dtype, name):
+            return scores.tile(shape, dtype, name=name, offset=4 * S * t + at, align_bytes=64)
+
+        def staging(b, width):
+            if b == 0:
+                return stage.tile([P, width], BF16, name="grouped", tag="grouped", align_bytes=64)
+            return late.tile([P, width], BF16, name="late_grouped", tag="late", align_bytes=64)
+
+        def quant_w1(a, b, grouped):
+            if b == 0:
+                w1_c[a, b] = keep.tile([P, PASS], U32, name="w1_c%d_%d" % (a, b), align_bytes=64)
+                w1_s[a, b] = keep.tile([P, PASS], U8, name="w1_s%d_%d" % (a, b), align_bytes=64)
+            else:
+                w1_c[a, b] = on_scores(a, 0, [P, PASS], U32, "w1_c%d_%d" % (a, b))
+                w1_s[a, b] = on_scores(a, 4 * PASS, [P, PASS], U8, "w1_s%d_%d" % (a, b))
+            nc.vector.quantize_mx(out=w1_c[a, b][:].bitcast(FP8X4), scales=w1_s[a, b][:], in_=grouped[:])
+
+        def round_w1(a, b, raw):
+            grouped = staging(b, PACK * PASS)
+            nc.scalar.copy(
+                out=grouped[:].rearrange("p (t m j) -> p m t j", t=PACK, j=PACK),
+                in_=raw[:].rearrange("p j (m t) -> p m t j", t=PACK),
+            )
+            return grouped
+
+        def round_w3(piece):
+            b, c = divmod(piece, 2)
+            raw = stage.tile([P, PACK, W3_PIECE], F32, name="raw3", tag="raw")
+            src = w3[PASS * b : PASS * (b + 1), W3_PIECE * c : W3_PIECE * (c + 1)]
+            nc.sync.dma_start(out=raw[:], in_=src.rearrange("(p j) c -> p j c", j=PACK))
+            grouped = staging(1, PACK * W3_PIECE)
+            nc.scalar.copy(
+                out=grouped[:].rearrange("p (c e j) -> p c j e", e=PACK, j=PACK),
+                in_=raw[:].rearrange("p j (c e) -> p c j e", e=PACK),
+            )
+            return grouped
+
+        def quant_w3(piece, grouped):
+            t = KP + piece
+            w3_c[piece] = on_scores(t, 0, [P, W3_PIECE], U32, "w3_c%d" % piece)
+            w3_s[piece] = on_scores(t, 4 * W3_PIECE, [P, W3_PIECE], U8, "w3_s%d" % piece)
+            nc.vector.quantize_mx(out=w3_c[piece][:].bitcast(FP8X4), scales=w3_s[piece][:], in_=grouped[:])
+
+        def load_wgs(i, cols):
+            src = wgs.rearrange("(q i) j -> i q j", i=PACK)[i]
+            for quadrant in (0, 2, 1, 3):
+                nc.sync.dma_start(out=wgs_t[i][32 * quadrant : 32 * quadrant + 32, cols], in_=src[:, cols])
+
+        def load_room(t, cols):
+            nc.sync.dma_start(out=room_t[t][:, cols], in_=rows(room, t)[:, cols])
+
+        def load_page(t):
+            page_t[t] = pages.tile([P, T2], F32, name="page", tag="page")
+            nc.sync.dma_start(out=page_t[t][:], in_=rows(page0, t))
+
+        def first_product(t):
+            b, i = divmod(t, PACK)
+            cols = slice(P * i, P * (i + 1))
+            for c in range(2):
+                acc1[t, c] = psum.tile([P, BANK], F32, name="acc1", tag="bank%d" % ((2 * t - 2 + c) % 8 if t < PACK else 6 + c))
+                for a in range(KP):
+                    nc.tensor.matmul_mx(
+                        out=acc1[t, c][:],
+                        lhsT=w1_c[a, b][:, cols].bitcast(FP8X4),
+                        lhsT_scale=w1_s[a, b][:, cols],
+                        rhs=v_w[a][c][:].bitcast(FP8X4),
+                        rhs_scale=v_s[4 * a : P, BANK * c : BANK * (c + 1)],
+                        start=(a == 0),
+                        stop=(a == KP - 1),
+                    )
+
+        def new_scores(t):
+            h_t[t] = on_scores(t, 0, [P, S], F32, "h%d" % t)
+            h = h_t[t]
+            if t == 0:
+                for c in range(2):
+                    rw = room_t[t][:, halves[c]]
+                    nc.gpsimd.tensor_tensor(out=rw, in0=rw, in1=wgs_t[0][:, halves[c]], op=ALU.mult)
+                    nc.vector.tensor_tensor(out=h[:, halves[c]], in0=acc1[t, c][:], in1=rw, op=ALU.mult)
+            else:
+                for c in range(2):
+                    nc.scalar.copy(out=h[:, halves[c]], in_=acc1[t, c][:])
+                nc.gpsimd.tensor_tensor(out=h[:], in0=h[:], in1=room_t[t][:], op=ALU.mult)
+                nc.gpsimd.tensor_tensor(out=h[:], in0=h[:], in1=wgs_t[t % PACK][:], op=ALU.mult)
+
+        def scatter(t):
+            if t == 0:
+                for c in range(2):
+                    nc.vector.tensor_copy(out=page_t[t][:].indirect(idx2[:, 32 * c : 32 * c + 32]), in_=h_t[t][:, halves[c]])
+            else:
+                nc.vector.tensor_copy(out=page_t[t][:].indirect(idx2[:]), in_=h_t[t][:])
+
+        def row_max(t):
+            top[t] = late.tile([P, 1], F32, name="top", tag="late", align_bytes=64)
+            nc.vector.tensor_reduce(out=top[t][:], in_=page_t[t][:], axis=AXIS.X, op=ALU.max)
+
+        def look(t):
+            b, i = divmod(t, PACK)
+            col = slice(t, t + 1)
+            nc.scalar.activation(out=bias[:, col], in_=top[t][:], func=ACT.Copy, scale=slope[:, col])
+            x = work.tile([P, M], F32, name="x", tag="x")
+            nc.scalar.activation(
+                out=x[:], in_=page_t[t][:].indirect(idx3[:]), func=ACT.Sigmoid, bias=bias[:, col], scale=vec["sharp"][:, col]
+            )
+            if i == 0:
+                y_bf[b] = work.tile([P, M, PACK], BF16, name="y_bf", tag="y_bf", align_bytes=64)
+            if t == TILES - 1:
+                nc.vector.tensor_scalar(
+                    out=y_bf[b][:, :, i], in0=x[:], scalar1=vec["least"][:, col], scalar2=vec["gain"][:, col],
+                    op0=ALU.max, op1=ALU.mult,
+                )
+            else:
+                above = work.tile([P, M], F32, name="above", tag="above")
+                nc.scalar.activation(out=above[:], in_=x[:], func=ACT.Relu, bias=neg_least[:, col])
+                nc.scalar.activation(
+                    out=y_bf[b][:, :, i], in_=above[:], func=ACT.Identity, bias=floor[:, col], scale=vec["gain"][:, col]
+                )
+
+        def quant_y(b):
+            y_c[b] = on_scores(PACK + 3 * b, 4 * M, [P, M], U32, "y_c%d" % b)
+            y_s[b] = keep.tile([P, M], U8, name="y_s%d" % b, align_bytes=64)
+            nc.vector.quantize_mx(
+                out=y_c[b][:].bitcast(FP8X4), scales=y_s[b][:], in_=y_bf[b][:].rearrange("p m i -> p (m i)")
+            )
+
+        def second_pass(n, b):
+            cols = slice(P * n, P * (n + 1))
+            piece = 2 * b + n // 3
+            cols3 = slice(P * (n % 3), P * (n % 3 + 1))
+            if b == 0:
+                for which in range(2):
+                    acc2[n, which] = psum.tile([P, M], F32, name="acc2", tag="bank%d" % ((2 * n + which) % 8))
+            nc.tensor.matmul_mx(
+                out=acc2[n, 0][:],
+                lhsT=w4_w[:, b, 2 * P * n : 2 * P * (n + 1)].bitcast(FP4X4),
+                lhsT_scale=w4_s[:, b, cols],
+                rhs=y_c[b][:].bitcast(FP8X4),
+                rhs_scale=y_s[b][:],
+                start=(b == 0),
+                stop=(b == HP - 1),
+            )
+            nc.tensor.matmul_mx(
+                out=acc2[n, 1][:],
+                lhsT=w3_c[piece][:, cols3].bitcast(FP8X4),
+                lhsT_scale=w3_s[piece][:, cols3],
+                rhs=y_c[b][:].bitcast(FP8X4),
+                rhs_scale=y_s[b][:],
+                start=(b == 0),
+                stop=(b == HP - 1),
+            )
+
+        def finish(n):
+            res = bal_t[n]
+            nc.vector.tensor_tensor(out=res[:], in0=acc2[n, 0][:], in1=res[:], op=ALU.mult)
+            if n < 4:
+                other = work.tile([P, M], F32, name="other", tag="other")
+                nc.scalar.copy(out=other[:], in_=acc2[n, 1][:])
+                nc.gpsimd.tensor_tensor(out=res[:], in0=res[:], in1=other[:], op=ALU.add)
+            else:
+                nc.vector.tensor_tensor(out=res[:], in0=acc2[n, 1][:], in1=res[:], op=ALU.add)
+            nc.sync.dma_start(out=out[P * n : P * (n + 1), :], in_=res[:])
+
+        vec = {}
+
+        def load_vec(name, ap):
+            vec3 = keep.tile([P, HP, PACK], F32, name="vec_" + name)
+            nc.sync.dma_start(out=vec3[:], in_=ap.rearrange("(b p i) -> p b i", b=HP, i=PACK))
+            vec[name] = vec3[:].rearrange("p b i -> p (b i)")
+
+        nc.gpsimd.memset(tab_s[:].bitcast(I32), 0)
+        nc.sync.dma_start(out=idx[:], in_=offs)
+        nc.sync.dma_start(out=idx2[:], in_=offs2)
+        nc.sync.dma_start(out=idx3[:], in_=offs3)
+        load_vec("sharp", sharp)
+        load_vec("share", share)
+        load_vec("least", least)
+        load_tab(0)
+        raw00 = load_w1(0, 0)
+        for q in range(4):
+            nc.sync.dma_start(
+                out=tab_s[32 * q : 32 * q + 4 * KP, :].bitcast(I32), in_=tab_scales[:, 4 * q : 4 * q + 4, :].bitcast(I32)
+            )
+        raw10 = load_w1(1, 0)
+        load_tab(1)
+        raw20 = load_w1(2, 0)
+        load_tab(2)
+        room_t[0] = stage.tile([P, S], F32, name="room", tag="room")
+        load_room(0, halves[0])
+        load_wgs(0, halves[0])
+        load_page(0)
+        load_room(0, halves[1])
+        load_wgs(0, halves[1])
+
+        nc.vector.tensor_copy(out=v_s[:], in_=tab_s[:].indirect(idx[:]))
+        gather_words(0, 0)
+        gather_words(0, 1)
+        quant_w1(0, 0, round_w1(0, 0, raw00))
+        quant_w1(1, 0, round_w1(1, 0, raw10))
+        gather_words(1, 0)
+        gather_words(1, 1)
+        quant_w1(2, 0, round_w1(2, 0, raw20))
+        gather_words(2, 0)
+        gather_words(2, 1)
+
+        load_vec("gain", gain)
+        slope = keep.tile([P, TILES], F32, name="slope")
+        neg_least = keep.tile([P, TILES], F32, name="neg_least")
+        floor = keep.tile([P, TILES], F32, name="floor")
+        nc.gpsimd.tensor_tensor(out=slope[:], in0=vec["sharp"], in1=vec["share"], op=ALU.mult)
+        nc.gpsimd.tensor_scalar(out=slope[:], in0=slope[:], scalar1=-1.0, scalar2=0.0, op0=ALU.mult, op1=ALU.add)
+        nc.gpsimd.tensor_scalar(out=neg_least[:], in0=vec["least"], scalar1=-1.0, scalar2=0.0, op0=ALU.mult, op1=ALU.add)
+        nc.gpsimd.tensor_tensor(out=floor[:], in0=vec["gain"], in1=vec["least"], op=ALU.mult)
+
+        w4_w = keep.tile([P, HP, 2 * N], U8, name="w4_w", align_bytes=64)
+        w4_s = keep.tile([P, HP, N], U8, name="w4_s", align_bytes=64)
+        nc.gpsimd.memset(w4_s[:].bitcast(I32), 0)
+
+        first_product(0)
+        new_scores(0)
+        for t in range(TILES):
+            nxt = t + 1
+            if t < KP:
+                grouped = round_w1(t, 1, load_w1(t, 1))
+            elif nxt < TILES:
+                grouped = round_w3(t - KP)
+            if t == 3:
+                nc.sync.dma_start(out=w4_w[:].bitcast(I32), in_=w4_words.rearrange("b p c -> p b c").bitcast(I32))
+                for q in range(4):
+                    nc.sync.dma_start(
+                        out=w4_s[32 * q : 32 * q + 4, :, :].bitcast(I32),
+                        in_=w4_scales[:, 4 * q : 4 * q + 4, :].rearrange("b r c -> r b c").bitcast(I32),
+                    )
+            scatter(t)
+            if t < KP:
+                quant_w1(t, 1, grouped)
+            elif nxt < TILES:
+                quant_w3(t - KP, grouped)
+            if nxt < TILES:
+                room_t[nxt] = stage.tile([P, S], F32, name="room", tag="room")
+                load_room(nxt, whole)
+                if nxt < PACK:
+                    load_wgs(nxt, whole)
+                load_page(nxt)
+                first_product(nxt)
+                new_scores(nxt)
+            else:
+                second_pass(3, 0)
+            if t == 6:
+                for n in range(NT):
+                    bal_t[n] = keep.tile([P, M], F32, name="bal%d" % n)
+                    nc.sync.dma_start(out=bal_t[n][:], in_=bal[P * n : P * (n + 1), :])
+            if t == PACK:
+                quant_y(0)
+                for n in range(3):
+                    second_pass(n, 0)
+            row_max(t)
+            look(t)
+
+        quant_y(1)
+        for n in range(NT):
+            if n >= 4:
+                second_pass(n, 0)
+            second_pass(n, 1)
+            finish(n)

@@ -67,7 +67,7 @@ def tile_list_box_placement_balance_kernel(
         acc1 = {}
         acc2 = {}
         bal_t = {}
-        top = {}
+        top = keep.tile([P, TILES], F32, name="top")
         bias = keep.tile([P, TILES], F32, name="bias")
 
         def rows(ap, t):
@@ -89,10 +89,10 @@ def tile_list_box_placement_balance_kernel(
         def on_scores(t, at, shape, dtype, name):
             return scores.tile(shape, dtype, name=name, offset=4 * S * t + at, align_bytes=64)
 
-        def staging(b, width):
-            if b == 0:
+        def staging(t, width):
+            if t is None:
                 return stage.tile([P, width], BF16, name="grouped", tag="grouped", align_bytes=64)
-            return late.tile([P, width], BF16, name="late_grouped", tag="late", align_bytes=64)
+            return late.tile([P, width], BF16, name="late_grouped", tag="late%d" % (t % 2), align_bytes=64)
 
         def quant_w1(a, b, grouped):
             if b == 0:
@@ -104,7 +104,7 @@ def tile_list_box_placement_balance_kernel(
             nc.vector.quantize_mx(out=w1_c[a, b][:].bitcast(FP8X4), scales=w1_s[a, b][:], in_=grouped[:])
 
         def round_w1(a, b, raw):
-            grouped = staging(b, PACK * PASS)
+            grouped = staging(a if b else None, PACK * PASS)
             nc.scalar.copy(
                 out=grouped[:].rearrange("p (t m j) -> p m t j", t=PACK, j=PACK),
                 in_=raw[:].rearrange("p j (m t) -> p m t j", t=PACK),
@@ -116,7 +116,7 @@ def tile_list_box_placement_balance_kernel(
             raw = stage.tile([P, PACK, W3_PIECE], F32, name="raw3", tag="raw")
             src = w3[PASS * b : PASS * (b + 1), W3_PIECE * c : W3_PIECE * (c + 1)]
             nc.sync.dma_start(out=raw[:], in_=src.rearrange("(p j) c -> p j c", j=PACK))
-            grouped = staging(1, PACK * W3_PIECE)
+            grouped = staging(KP + piece, PACK * W3_PIECE)
             nc.scalar.copy(
                 out=grouped[:].rearrange("p (c e j) -> p c j e", e=PACK, j=PACK),
                 in_=raw[:].rearrange("p j (c e) -> p c j e", e=PACK),
@@ -168,8 +168,13 @@ def tile_list_box_placement_balance_kernel(
             else:
                 for c in range(2):
                     nc.scalar.copy(out=h[:, halves[c]], in_=acc1[t, c][:])
-                nc.gpsimd.tensor_tensor(out=h[:], in0=h[:], in1=room_t[t][:], op=ALU.mult)
-                nc.gpsimd.tensor_tensor(out=h[:], in0=h[:], in1=wgs_t[t % PACK][:], op=ALU.mult)
+                if t == 1:
+                    nc.gpsimd.tensor_tensor(out=h[:], in0=h[:], in1=room_t[t][:], op=ALU.mult)
+                    nc.gpsimd.tensor_tensor(out=h[:], in0=h[:], in1=wgs_t[t][:], op=ALU.mult)
+                else:
+                    rw = late.tile([P, S], F32, name="rw", tag="late%d" % (t % 2), align_bytes=64)
+                    nc.gpsimd.tensor_tensor(out=rw[:], in0=room_t[t][:], in1=wgs_t[t % PACK][:], op=ALU.mult)
+                    nc.gpsimd.tensor_tensor(out=h[:], in0=h[:], in1=rw[:], op=ALU.mult)
 
         def scatter(t):
             if t == 0:
@@ -179,13 +184,12 @@ def tile_list_box_placement_balance_kernel(
                 nc.vector.tensor_copy(out=page_t[t][:].indirect(idx2[:]), in_=h_t[t][:])
 
         def row_max(t):
-            top[t] = late.tile([P, 1], F32, name="top", tag="late", align_bytes=64)
-            nc.vector.tensor_reduce(out=top[t][:], in_=page_t[t][:], axis=AXIS.X, op=ALU.max)
+            nc.vector.tensor_reduce(out=top[:, t : t + 1], in_=page_t[t][:], axis=AXIS.X, op=ALU.max)
 
         def look(t):
             b, i = divmod(t, PACK)
             col = slice(t, t + 1)
-            nc.scalar.activation(out=bias[:, col], in_=top[t][:], func=ACT.Copy, scale=slope[:, col])
+            nc.scalar.activation(out=bias[:, col], in_=top[:, col], func=ACT.Copy, scale=slope[:, col])
             x = work.tile([P, M], F32, name="x", tag="x")
             nc.scalar.activation(
                 out=x[:], in_=page_t[t][:].indirect(idx3[:]), func=ACT.Sigmoid, bias=bias[:, col], scale=vec["sharp"][:, col]
@@ -205,7 +209,7 @@ def tile_list_box_placement_balance_kernel(
                 )
 
         def quant_y(b):
-            y_c[b] = on_scores(PACK + 3 * b, 4 * M, [P, M], U32, "y_c%d" % b)
+            y_c[b] = on_scores(TILES - 1, 4 * M * b, [P, M], U32, "y_c%d" % b)
             y_s[b] = keep.tile([P, M], U8, name="y_s%d" % b, align_bytes=64)
             nc.vector.quantize_mx(
                 out=y_c[b][:].bitcast(FP8X4), scales=y_s[b][:], in_=y_bf[b][:].rearrange("p m i -> p (m i)")
@@ -319,6 +323,11 @@ def tile_list_box_placement_balance_kernel(
                         in_=w4_scales[:, 4 * q : 4 * q + 4, :].rearrange("b r c -> r b c").bitcast(I32),
                     )
             scatter(t)
+            if nxt == TILES:
+                quant_y(0)
+                for n in range(4):
+                    second_pass(n, 0)
+            row_max(t)
             if t < KP:
                 quant_w1(t, 1, grouped)
             elif nxt < TILES:
@@ -331,17 +340,10 @@ def tile_list_box_placement_balance_kernel(
                 load_page(nxt)
                 first_product(nxt)
                 new_scores(nxt)
-            else:
-                second_pass(3, 0)
             if t == 6:
                 for n in range(NT):
                     bal_t[n] = keep.tile([P, M], F32, name="bal%d" % n)
                     nc.sync.dma_start(out=bal_t[n][:], in_=bal[P * n : P * (n + 1), :])
-            if t == PACK:
-                quant_y(0)
-                for n in range(3):
-                    second_pass(n, 0)
-            row_max(t)
             look(t)
 
         quant_y(1)

@@ -1,6 +1,7 @@
 from contextlib import ExitStack
 
 import concourse.mybir as mybir
+from concourse.masks import make_identity
 
 K, H, N, T, S, T2, M = 1536, 1024, 768, 2048, 1024, 2048, 512
 FLOPS = 2 * K * H * S + 2 * 2 * H * N * M
@@ -23,7 +24,7 @@ PASS = P * PACK
 BANK = 512
 KP = K // PASS
 HP = H // PASS
-TILES = HP * PACK
+TILES = H // P
 NT = N // P
 W3_PIECE = 384
 
@@ -37,102 +38,122 @@ def tile_list_box_placement_balance_kernel(
         lists = ctx.enter_context(tc.tile_pool(name="lists", bufs=1))
         keep = ctx.enter_context(tc.tile_pool(name="keep", bufs=1))
         stage = ctx.enter_context(tc.tile_pool(name="stage", bufs=3))
-        pages = ctx.enter_context(tc.tile_pool(name="pages", bufs=5))
+        pages = ctx.enter_context(tc.tile_pool(name="pages", bufs=4))
         work = ctx.enter_context(tc.tile_pool(name="work", bufs=2))
-        late = ctx.enter_context(tc.tile_pool(name="late", bufs=1))
         scores = ctx.enter_context(tc.tile_pool(name="scores", bufs=1))
+        table = ctx.enter_context(tc.tile_pool(name="table", bufs=1))
         psum = ctx.enter_context(tc.psum_pool(name="psum", bufs=1))
 
         idx = lists.tile([P, S // 16], U16, name="idx")
         idx2 = lists.tile([P, S // 16], U16, name="idx2")
         idx3 = lists.tile([P, M // 16], U16, name="idx3")
 
-        tab_w = [keep.tile([P, T], I32, name="tab_w%d" % a) for a in range(KP)]
+        tab_w = [table.tile([P, T], I32, name="tab_w%d" % a, offset=4 * T * a) for a in range(KP)]
         tab_s = keep.tile([P, T], U8, name="tab_s")
         v_w = [[keep.tile([P, BANK], U32, name="v_w%d_%d" % (a, c), align_bytes=64) for c in range(2)] for a in range(KP)]
         v_s = keep.tile([P, S], U8, name="v_s", align_bytes=64)
+        wgs_sb = keep.tile([P, S], F32, name="wgs_sb")
+        wgs_t = {t: wgs_sb for t in range(PACK)}
+        y_bf = {}
+        w4_w = keep.tile([P, HP, 2 * N], U8, name="w4_w", align_bytes=64)
+        w4_s = keep.tile([P, HP, N], U8, name="w4_s", align_bytes=64)
+        top = keep.tile([P, TILES], F32, name="top")
+        bias = keep.tile([P, TILES], F32, name="bias")
         w1_c = {}
         w1_s = {}
+        lhs = {}
         w3_c = {}
         w3_s = {}
+        y_plain = {}
         y_c = {}
         y_s = {}
-        y_bf = {}
         room_t = {}
         page_t = {}
         h_t = {}
-        wgs_t = [keep.tile([P, S], F32, name="wgs%d" % i) for i in range(PACK)]
-        halves = [slice(BANK * c, BANK * (c + 1)) for c in range(2)]
-        whole = slice(0, S)
         acc1 = {}
         acc2 = {}
         bal_t = {}
-        top = keep.tile([P, TILES], F32, name="top")
-        bias = keep.tile([P, TILES], F32, name="bias")
-
-        def rows(ap, t):
-            b, i = divmod(t, PACK)
-            return ap.rearrange("(b p i) c -> b i p c", b=HP, i=PACK)[b, i]
-
-        def load_tab(a):
-            nc.sync.dma_start(out=tab_w[a][:], in_=tab_words[a].rearrange("p t i -> p (t i)").bitcast(I32))
-
-        def gather_words(a, c):
-            nc.vector.tensor_copy(out=v_w[a][c][:], in_=tab_w[a][:].bitcast(U32).indirect(idx[:, 32 * c : 32 * c + 32]))
-
-        def load_w1(a, b):
-            raw = stage.tile([P, PACK, PASS], F32, name="raw", tag="raw")
-            src = w1[PASS * a : PASS * (a + 1), PASS * b : PASS * (b + 1)]
-            nc.sync.dma_start(out=raw[:], in_=src.rearrange("(p j) c -> p j c", j=PACK))
-            return raw
+        vec = {}
+        halves = [slice(BANK * c, BANK * (c + 1)) for c in range(2)]
+        whole = slice(0, S)
 
         def on_scores(t, at, shape, dtype, name):
             return scores.tile(shape, dtype, name=name, offset=4 * S * t + at, align_bytes=64)
 
-        def staging(t, width):
-            if t is None:
-                return stage.tile([P, width], BF16, name="grouped", tag="grouped", align_bytes=64)
-            return late.tile([P, width], BF16, name="late_grouped", tag="late%d" % (t % 2), align_bytes=64)
+        def load_tab(a, pieces):
+            src = tab_words[a].rearrange("p t i -> p (t i)").bitcast(I32)
+            for c0 in range(0, T, T // pieces):
+                cols = slice(c0, c0 + T // pieces)
+                nc.sync.dma_start(out=tab_w[a][:, cols], in_=src[:, cols])
 
-        def quant_w1(a, b, grouped):
-            if b == 0:
-                w1_c[a, b] = keep.tile([P, PASS], U32, name="w1_c%d_%d" % (a, b), align_bytes=64)
-                w1_s[a, b] = keep.tile([P, PASS], U8, name="w1_s%d_%d" % (a, b), align_bytes=64)
+        def gather_words(a, c):
+            nc.vector.tensor_copy(out=v_w[a][c][:], in_=tab_w[a][:].bitcast(U32).indirect(idx[:, 32 * c : 32 * c + 32]))
+
+        def interleaved(out, in_):
+            return (
+                out.rearrange("p (c e j) -> p c j e", e=PACK, j=PACK),
+                in_.rearrange("p j (c e) -> p c j e", e=PACK),
+            )
+
+        def round_w1(t):
+            raw = stage.tile([P, KP, PACK, P], F32, name="raw1", tag="raw", bufs=4)
+            grouped = stage.tile([P, KP * PASS], BF16, name="grouped1", tag="grouped", align_bytes=64)
+            for a in range(KP):
+                src = w1[PASS * a : PASS * (a + 1), P * t : P * (t + 1)]
+                nc.sync.dma_start(out=raw[:, a, :, :], in_=src.rearrange("(p j) c -> p j c", j=PACK))
+                nc.scalar.copy(*interleaved(grouped[:, PASS * a : PASS * (a + 1)], raw[:, a, :, :]))
+            return grouped
+
+        def quant_w1(t, grouped):
+            if t == 0:
+                w1_c[t] = keep.tile([P, KP * P], U32, name="w1_c0", align_bytes=64)
+            elif t == 1:
+                w1_c[t] = on_scores(0, 0, [P, KP * P], U32, "w1_c1")
             else:
-                w1_c[a, b] = on_scores(a, 0, [P, PASS], U32, "w1_c%d_%d" % (a, b))
-                w1_s[a, b] = on_scores(a, 4 * PASS, [P, PASS], U8, "w1_s%d_%d" % (a, b))
-            nc.vector.quantize_mx(out=w1_c[a, b][:].bitcast(FP8X4), scales=w1_s[a, b][:], in_=grouped[:])
+                w1_c[t] = on_scores(t - 2, 2 * S, [P, KP * P], U32, "w1_c%d" % t)
+            w1_s[t] = keep.tile([P, KP * P], U8, name="w1_s%d" % t, align_bytes=64)
+            nc.vector.quantize_mx(out=w1_c[t][:].bitcast(FP8X4), scales=w1_s[t][:], in_=grouped[:])
+            for a in range(KP):
+                lhs[t, a] = (w1_c[t][:, P * a : P * (a + 1)], w1_s[t][:, P * a : P * (a + 1)])
 
-        def round_w1(a, b, raw):
-            grouped = staging(a if b else None, PACK * PASS)
+        def load_w1_wide(a):
+            raw = stage.tile([P, PACK, PASS], F32, name="raw2", tag="raw", bufs=4)
+            nc.sync.dma_start(out=raw[:], in_=w1[PASS * a : PASS * (a + 1), PASS:].rearrange("(p j) c -> p j c", j=PACK))
+            return raw
+
+        def round_w1_wide(raw):
+            grouped = stage.tile([P, PACK * PASS], BF16, name="grouped2", tag="grouped", align_bytes=64)
             nc.scalar.copy(
-                out=grouped[:].rearrange("p (t m j) -> p m t j", t=PACK, j=PACK),
-                in_=raw[:].rearrange("p j (m t) -> p m t j", t=PACK),
+                out=grouped[:].rearrange("p (i q j) -> p q i j", i=PACK, j=PACK),
+                in_=raw[:].rearrange("p j (q i) -> p q i j", i=PACK),
             )
             return grouped
+
+        def quant_w1_wide(a, host, at, grouped):
+            codes = on_scores(host, at, [P, PASS], U32, "w1w_c%d" % a)
+            planes = keep.tile([P, PASS], U8, name="w1w_s%d" % a, align_bytes=64)
+            nc.vector.quantize_mx(out=codes[:].bitcast(FP8X4), scales=planes[:], in_=grouped[:])
+            for i in range(PACK):
+                lhs[PACK + i, a] = (codes[:, P * i : P * (i + 1)], planes[:, P * i : P * (i + 1)])
 
         def round_w3(piece):
             b, c = divmod(piece, 2)
-            raw = stage.tile([P, PACK, W3_PIECE], F32, name="raw3", tag="raw")
+            raw = stage.tile([P, PACK, W3_PIECE], F32, name="raw3", tag="raw3", bufs=2)
             src = w3[PASS * b : PASS * (b + 1), W3_PIECE * c : W3_PIECE * (c + 1)]
             nc.sync.dma_start(out=raw[:], in_=src.rearrange("(p j) c -> p j c", j=PACK))
-            grouped = staging(KP + piece, PACK * W3_PIECE)
-            nc.scalar.copy(
-                out=grouped[:].rearrange("p (c e j) -> p c j e", e=PACK, j=PACK),
-                in_=raw[:].rearrange("p j (c e) -> p c j e", e=PACK),
-            )
+            grouped = stage.tile([P, PACK * W3_PIECE], BF16, name="grouped3", tag="grouped3", align_bytes=64)
+            nc.scalar.copy(*interleaved(grouped[:], raw[:]))
             return grouped
 
-        def quant_w3(piece, grouped):
-            t = KP + piece
-            w3_c[piece] = on_scores(t, 0, [P, W3_PIECE], U32, "w3_c%d" % piece)
-            w3_s[piece] = on_scores(t, 4 * W3_PIECE, [P, W3_PIECE], U8, "w3_s%d" % piece)
+        def quant_w3(piece, host, at, grouped):
+            w3_c[piece] = on_scores(host, at, [P, W3_PIECE], U32, "w3_c%d" % piece)
+            w3_s[piece] = keep.tile([P, W3_PIECE], U8, name="w3_s%d" % piece, align_bytes=64)
             nc.vector.quantize_mx(out=w3_c[piece][:].bitcast(FP8X4), scales=w3_s[piece][:], in_=grouped[:])
 
-        def load_wgs(i, cols):
-            src = wgs.rearrange("(q i) j -> i q j", i=PACK)[i]
-            for quadrant in (0, 2, 1, 3):
-                nc.sync.dma_start(out=wgs_t[i][32 * quadrant : 32 * quadrant + 32, cols], in_=src[:, cols])
+        def rows(ap, t):
+            if t < PACK:
+                return ap[P * t : P * (t + 1), :]
+            return ap[PASS:, :].rearrange("(p i) c -> i p c", i=PACK)[t - PACK]
 
         def load_room(t, cols):
             nc.sync.dma_start(out=room_t[t][:, cols], in_=rows(room, t)[:, cols])
@@ -141,45 +162,78 @@ def tile_list_box_placement_balance_kernel(
             page_t[t] = pages.tile([P, T2], F32, name="page", tag="page")
             nc.sync.dma_start(out=page_t[t][:], in_=rows(page0, t))
 
+        def load_wgs_dealt(i):
+            wgs_t[PACK + i] = table.tile([P, S], F32, name="wgs%d" % i, offset=4 * S * i)
+            src = wgs.rearrange("(q i) j -> i q j", i=PACK)[i]
+            for quadrant in (0, 2, 1, 3):
+                nc.sync.dma_start(out=wgs_t[PACK + i][32 * quadrant : 32 * quadrant + 32, :], in_=src)
+
+        def load_row_values(b):
+            given = (("sharp", sharp), ("share", share), ("least", least), ("gain", gain))
+            per_row = {}
+            if b == 0:
+                as_rows = keep.tile([P, P], F32, name="as_rows")
+                identity = keep.tile([P, P], F32, name="identity")
+                nc.gpsimd.memset(as_rows[:], 0.0)
+                make_identity(nc, identity[:])
+                for n, (name, ap) in enumerate(given):
+                    nc.sync.dma_start(out=as_rows[PACK * n : PACK * (n + 1), :], in_=ap[:PASS].rearrange("(t p) -> t p", p=P))
+                turned = psum.tile([P, P], F32, name="turned", tag="bank5")
+                nc.tensor.transpose(turned[:], as_rows[:], identity[:])
+                as_cols = keep.tile([P, len(given) * PACK], F32, name="as_cols")
+                nc.scalar.copy(out=as_cols[:], in_=turned[:, : len(given) * PACK])
+                for n, (name, ap) in enumerate(given):
+                    per_row[name] = as_cols[:, PACK * n : PACK * (n + 1)]
+            else:
+                for name, ap in given:
+                    loaded = keep.tile([P, PACK], F32, name=name)
+                    nc.sync.dma_start(out=loaded[:], in_=ap[PASS:].rearrange("(p i) -> p i", i=PACK))
+                    per_row[name] = loaded[:]
+            for name in ("slope", "neg_least", "floor"):
+                derived = keep.tile([P, PACK], F32, name="%s%d" % (name, b))
+                per_row[name] = derived[:]
+            slope = per_row["slope"]
+            nc.gpsimd.tensor_tensor(out=slope, in0=per_row["sharp"], in1=per_row["share"], op=ALU.mult)
+            nc.gpsimd.tensor_scalar(out=slope, in0=slope, scalar1=-1.0, scalar2=0.0, op0=ALU.mult, op1=ALU.add)
+            nc.gpsimd.tensor_scalar(
+                out=per_row["neg_least"], in0=per_row["least"], scalar1=-1.0, scalar2=0.0, op0=ALU.mult, op1=ALU.add
+            )
+            nc.gpsimd.tensor_tensor(out=per_row["floor"], in0=per_row["gain"], in1=per_row["least"], op=ALU.mult)
+            vec[b] = per_row
+
         def first_product(t):
-            b, i = divmod(t, PACK)
-            cols = slice(P * i, P * (i + 1))
             for c in range(2):
-                acc1[t, c] = psum.tile([P, BANK], F32, name="acc1", tag="bank%d" % ((2 * t - 2 + c) % 8 if t < PACK else 6 + c))
+                acc1[t, c] = psum.tile([P, BANK], F32, name="acc1", tag="bank%d" % (2 * (t % 2) + c))
                 for a in range(KP):
                     nc.tensor.matmul_mx(
                         out=acc1[t, c][:],
-                        lhsT=w1_c[a, b][:, cols].bitcast(FP8X4),
-                        lhsT_scale=w1_s[a, b][:, cols],
+                        lhsT=lhs[t, a][0].bitcast(FP8X4),
+                        lhsT_scale=lhs[t, a][1],
                         rhs=v_w[a][c][:].bitcast(FP8X4),
-                        rhs_scale=v_s[4 * a : P, BANK * c : BANK * (c + 1)],
+                        rhs_scale=v_s[4 * a : P, halves[c]],
                         start=(a == 0),
                         stop=(a == KP - 1),
                     )
 
         def new_scores(t):
-            h_t[t] = on_scores(t, 0, [P, S], F32, "h%d" % t)
-            h = h_t[t]
+            rw = room_t[t]
             if t == 0:
                 for c in range(2):
-                    rw = room_t[t][:, halves[c]]
-                    nc.gpsimd.tensor_tensor(out=rw, in0=rw, in1=wgs_t[0][:, halves[c]], op=ALU.mult)
-                    nc.vector.tensor_tensor(out=h[:, halves[c]], in0=acc1[t, c][:], in1=rw, op=ALU.mult)
+                    h_t[0, c] = on_scores(0, 2 * S * c, [P, BANK], F32, "h0_%d" % c)
+                    nc.gpsimd.tensor_tensor(out=rw[:, halves[c]], in0=rw[:, halves[c]], in1=wgs_sb[:, halves[c]], op=ALU.mult)
+                    nc.vector.tensor_tensor(out=h_t[0, c][:], in0=acc1[t, c][:], in1=rw[:, halves[c]], op=ALU.mult)
             else:
+                h_t[t] = on_scores(t, 0, [P, S], F32, "h%d" % t)
+                nc.gpsimd.tensor_tensor(out=rw[:], in0=rw[:], in1=wgs_t[t][:], op=ALU.mult)
                 for c in range(2):
-                    nc.scalar.copy(out=h[:, halves[c]], in_=acc1[t, c][:])
-                if t == 1:
-                    nc.gpsimd.tensor_tensor(out=h[:], in0=h[:], in1=room_t[t][:], op=ALU.mult)
-                    nc.gpsimd.tensor_tensor(out=h[:], in0=h[:], in1=wgs_t[t][:], op=ALU.mult)
-                else:
-                    rw = late.tile([P, S], F32, name="rw", tag="late%d" % (t % 2), align_bytes=64)
-                    nc.gpsimd.tensor_tensor(out=rw[:], in0=room_t[t][:], in1=wgs_t[t % PACK][:], op=ALU.mult)
-                    nc.gpsimd.tensor_tensor(out=h[:], in0=h[:], in1=rw[:], op=ALU.mult)
+                    h = h_t[t][:, halves[c]]
+                    nc.scalar.copy(out=h, in_=acc1[t, c][:])
+                    nc.gpsimd.tensor_tensor(out=h, in0=h, in1=rw[:, halves[c]], op=ALU.mult)
 
         def scatter(t):
             if t == 0:
                 for c in range(2):
-                    nc.vector.tensor_copy(out=page_t[t][:].indirect(idx2[:, 32 * c : 32 * c + 32]), in_=h_t[t][:, halves[c]])
+                    nc.vector.tensor_copy(out=page_t[t][:].indirect(idx2[:, 32 * c : 32 * c + 32]), in_=h_t[0, c][:])
             else:
                 nc.vector.tensor_copy(out=page_t[t][:].indirect(idx2[:]), in_=h_t[t][:])
 
@@ -188,25 +242,40 @@ def tile_list_box_placement_balance_kernel(
 
         def look(t):
             b, i = divmod(t, PACK)
-            col = slice(t, t + 1)
-            nc.scalar.activation(out=bias[:, col], in_=top[:, col], func=ACT.Copy, scale=slope[:, col])
+            col = slice(i, i + 1)
+            per_row = vec[b]
+            nc.scalar.activation(out=bias[:, t : t + 1], in_=top[:, t : t + 1], func=ACT.Copy, scale=per_row["slope"][:, col])
             x = work.tile([P, M], F32, name="x", tag="x")
             nc.scalar.activation(
-                out=x[:], in_=page_t[t][:].indirect(idx3[:]), func=ACT.Sigmoid, bias=bias[:, col], scale=vec["sharp"][:, col]
+                out=x[:], in_=page_t[t][:].indirect(idx3[:]), func=ACT.Sigmoid,
+                bias=bias[:, t : t + 1], scale=per_row["sharp"][:, col],
             )
-            if i == 0:
-                y_bf[b] = work.tile([P, M, PACK], BF16, name="y_bf", tag="y_bf", align_bytes=64)
+            if b == 0:
+                y_plain[t] = keep.tile([P, M], BF16, name="y_plain%d" % t)
+                y = y_plain[t][:]
+            else:
+                if i == 0:
+                    y_bf[b] = keep.tile([P, M, PACK], BF16, name="y_bf1", align_bytes=64)
+                y = y_bf[b][:, :, i]
             if t == TILES - 1:
                 nc.vector.tensor_scalar(
-                    out=y_bf[b][:, :, i], in0=x[:], scalar1=vec["least"][:, col], scalar2=vec["gain"][:, col],
+                    out=y, in0=x[:], scalar1=per_row["least"][:, col], scalar2=per_row["gain"][:, col],
                     op0=ALU.max, op1=ALU.mult,
                 )
             else:
                 above = work.tile([P, M], F32, name="above", tag="above")
-                nc.scalar.activation(out=above[:], in_=x[:], func=ACT.Relu, bias=neg_least[:, col])
+                nc.scalar.activation(out=above[:], in_=x[:], func=ACT.Relu, bias=per_row["neg_least"][:, col])
                 nc.scalar.activation(
-                    out=y_bf[b][:, :, i], in_=above[:], func=ACT.Identity, bias=floor[:, col], scale=vec["gain"][:, col]
+                    out=y, in_=above[:], func=ACT.Identity, bias=per_row["floor"][:, col], scale=per_row["gain"][:, col]
                 )
+
+        def deal_y():
+            dealt = table.tile([P, PACK, M], BF16, name="y_dealt", offset=4 * S * PACK)
+            for t in range(PACK):
+                for i in range(PACK):
+                    nc.sync.dma_start(out=dealt[32 * t : 32 * t + 32, i, :], in_=y_plain[t][i:P:PACK, :])
+            y_bf[0] = keep.tile([P, M, PACK], BF16, name="y_bf0", align_bytes=64)
+            nc.scalar.copy(*interleaved(y_bf[0][:].rearrange("p m i -> p (m i)"), dealt[:]))
 
         def quant_y(b):
             y_c[b] = on_scores(TILES - 1, 4 * M * b, [P, M], U32, "y_c%d" % b)
@@ -252,98 +321,109 @@ def tile_list_box_placement_balance_kernel(
                 nc.vector.tensor_tensor(out=res[:], in0=acc2[n, 1][:], in1=res[:], op=ALU.add)
             nc.sync.dma_start(out=out[P * n : P * (n + 1), :], in_=res[:])
 
-        vec = {}
-
-        def load_vec(name, ap):
-            vec3 = keep.tile([P, HP, PACK], F32, name="vec_" + name)
-            nc.sync.dma_start(out=vec3[:], in_=ap.rearrange("(b p i) -> p b i", b=HP, i=PACK))
-            vec[name] = vec3[:].rearrange("p b i -> p (b i)")
-
         nc.gpsimd.memset(tab_s[:].bitcast(I32), 0)
+        nc.gpsimd.memset(w4_s[:].bitcast(I32), 0)
         nc.sync.dma_start(out=idx[:], in_=offs)
-        nc.sync.dma_start(out=idx2[:], in_=offs2)
-        nc.sync.dma_start(out=idx3[:], in_=offs3)
-        load_vec("sharp", sharp)
-        load_vec("share", share)
-        load_vec("least", least)
-        load_tab(0)
-        raw00 = load_w1(0, 0)
+        load_tab(0, 4)
+        grouped0 = round_w1(0)
         for q in range(4):
             nc.sync.dma_start(
                 out=tab_s[32 * q : 32 * q + 4 * KP, :].bitcast(I32), in_=tab_scales[:, 4 * q : 4 * q + 4, :].bitcast(I32)
             )
-        raw10 = load_w1(1, 0)
-        load_tab(1)
-        raw20 = load_w1(2, 0)
-        load_tab(2)
+        load_tab(1, 1)
+        load_tab(2, 1)
+        nc.vector.tensor_copy(out=v_s[:], in_=tab_s[:].indirect(idx[:]))
+        quant_w1(0, grouped0)
+        for a in range(KP):
+            for c in range(2):
+                gather_words(a, c)
         room_t[0] = stage.tile([P, S], F32, name="room", tag="room")
         load_room(0, halves[0])
-        load_wgs(0, halves[0])
+        nc.sync.dma_start(out=wgs_sb[:, halves[0]], in_=wgs[:, halves[0]])
+        nc.sync.dma_start(out=idx2[:], in_=offs2)
         load_page(0)
+        grouped1 = round_w1(1)
         load_room(0, halves[1])
-        load_wgs(0, halves[1])
-
-        nc.vector.tensor_copy(out=v_s[:], in_=tab_s[:].indirect(idx[:]))
-        gather_words(0, 0)
-        gather_words(0, 1)
-        quant_w1(0, 0, round_w1(0, 0, raw00))
-        quant_w1(1, 0, round_w1(1, 0, raw10))
-        gather_words(1, 0)
-        gather_words(1, 1)
-        quant_w1(2, 0, round_w1(2, 0, raw20))
-        gather_words(2, 0)
-        gather_words(2, 1)
-
-        load_vec("gain", gain)
-        slope = keep.tile([P, TILES], F32, name="slope")
-        neg_least = keep.tile([P, TILES], F32, name="neg_least")
-        floor = keep.tile([P, TILES], F32, name="floor")
-        nc.gpsimd.tensor_tensor(out=slope[:], in0=vec["sharp"], in1=vec["share"], op=ALU.mult)
-        nc.gpsimd.tensor_scalar(out=slope[:], in0=slope[:], scalar1=-1.0, scalar2=0.0, op0=ALU.mult, op1=ALU.add)
-        nc.gpsimd.tensor_scalar(out=neg_least[:], in0=vec["least"], scalar1=-1.0, scalar2=0.0, op0=ALU.mult, op1=ALU.add)
-        nc.gpsimd.tensor_tensor(out=floor[:], in0=vec["gain"], in1=vec["least"], op=ALU.mult)
-
-        w4_w = keep.tile([P, HP, 2 * N], U8, name="w4_w", align_bytes=64)
-        w4_s = keep.tile([P, HP, N], U8, name="w4_s", align_bytes=64)
-        nc.gpsimd.memset(w4_s[:].bitcast(I32), 0)
-
+        nc.sync.dma_start(out=wgs_sb[:, halves[1]], in_=wgs[:, halves[1]])
         first_product(0)
         new_scores(0)
-        for t in range(TILES):
-            nxt = t + 1
-            if t < KP:
-                grouped = round_w1(t, 1, load_w1(t, 1))
-            elif nxt < TILES:
-                grouped = round_w3(t - KP)
-            if t == 3:
+
+        def next_room(t):
+            room_t[t] = stage.tile([P, S], F32, name="room", tag="room")
+            load_room(t, whole)
+
+        def next_scores(t):
+            first_product(t)
+            new_scores(t)
+
+        scatter(0)
+        quant_w1(1, grouped1)
+        next_room(1)
+        grouped2 = round_w1(2)
+        nc.sync.dma_start(out=idx3[:], in_=offs3)
+        load_row_values(0)
+        load_page(1)
+        next_scores(1)
+        row_max(0)
+        quant_w1(2, grouped2)
+        look(0)
+
+        grouped3 = round_w1(3)
+        scatter(1)
+        next_room(2)
+        raw_wide = [load_w1_wide(0), load_w1_wide(1)]
+        load_page(2)
+        next_scores(2)
+        wide = [round_w1_wide(raw) for raw in raw_wide]
+        row_max(1)
+        quant_w1(3, grouped3)
+        look(1)
+
+        wide.append(round_w1_wide(load_w1_wide(2)))
+        scatter(2)
+        next_room(3)
+        load_wgs_dealt(0)
+        load_page(3)
+        next_scores(3)
+        row_max(2)
+        quant_w1_wide(0, 2, 0, wide[0])
+        quant_w1_wide(1, 2, 2 * S, wide[1])
+        quant_w1_wide(2, 1, 0, wide[2])
+        look(2)
+        load_row_values(1)
+
+        waiting = []
+        for t in range(KP, TILES):
+            scatter(t)
+            ready = waiting
+            waiting = []
+            if t + 1 < TILES:
+                next_room(t + 1)
+                load_page(t + 1)
+                next_scores(t + 1)
+            if t + 2 < TILES:
+                pieces = ([0], [1, 2], [3])[t - KP]
+                waiting = [(piece, round_w3(piece)) for piece in pieces]
+                load_wgs_dealt(t + 2 - PACK)
+            if t == TILES - 3:
+                deal_y()
+            row_max(t)
+            for n, (piece, grouped) in enumerate(ready):
+                quant_w3(piece, t, 2 * S * n, grouped)
+            if t == TILES - 2:
                 nc.sync.dma_start(out=w4_w[:].bitcast(I32), in_=w4_words.rearrange("b p c -> p b c").bitcast(I32))
                 for q in range(4):
                     nc.sync.dma_start(
                         out=w4_s[32 * q : 32 * q + 4, :, :].bitcast(I32),
                         in_=w4_scales[:, 4 * q : 4 * q + 4, :].rearrange("b r c -> r b c").bitcast(I32),
                     )
-            scatter(t)
-            if nxt == TILES:
-                quant_y(0)
-                for n in range(4):
-                    second_pass(n, 0)
-            row_max(t)
-            if t < KP:
-                quant_w1(t, 1, grouped)
-            elif nxt < TILES:
-                quant_w3(t - KP, grouped)
-            if nxt < TILES:
-                room_t[nxt] = stage.tile([P, S], F32, name="room", tag="room")
-                load_room(nxt, whole)
-                if nxt < PACK:
-                    load_wgs(nxt, whole)
-                load_page(nxt)
-                first_product(nxt)
-                new_scores(nxt)
-            if t == 6:
                 for n in range(NT):
                     bal_t[n] = keep.tile([P, M], F32, name="bal%d" % n)
                     nc.sync.dma_start(out=bal_t[n][:], in_=bal[P * n : P * (n + 1), :])
+            if t == TILES - 1:
+                quant_y(0)
+                for n in range(4):
+                    second_pass(n, 0)
             look(t)
 
         quant_y(1)

@@ -70,6 +70,7 @@ def tile_list_box_placement_balance_kernel(
         room_t = {}
         page_t = {}
         h_t = {}
+        x_t = {}
         acc1 = {}
         acc2 = {}
         bal_t = {}
@@ -95,12 +96,16 @@ def tile_list_box_placement_balance_kernel(
                 in_.rearrange("p j (c e) -> p c j e", e=PACK),
             )
 
-        def round_w1(t):
+        def load_w1(t):
             raw = stage.tile([P, KP, PACK, P], F32, name="raw1", tag="raw", bufs=4)
-            grouped = stage.tile([P, KP * PASS], BF16, name="grouped1", tag="grouped", align_bytes=64)
             for a in range(KP):
                 src = w1[PASS * a : PASS * (a + 1), P * t : P * (t + 1)]
                 nc.sync.dma_start(out=raw[:, a, :, :], in_=src.rearrange("(p j) c -> p j c", j=PACK))
+            return raw
+
+        def round_w1(t, raw):
+            grouped = stage.tile([P, KP * PASS], BF16, name="grouped1", tag="grouped", align_bytes=64)
+            for a in range(KP):
                 nc.scalar.copy(*interleaved(grouped[:, PASS * a : PASS * (a + 1)], raw[:, a, :, :]))
             return grouped
 
@@ -168,38 +173,32 @@ def tile_list_box_placement_balance_kernel(
             for quadrant in (0, 2, 1, 3):
                 nc.sync.dma_start(out=wgs_t[PACK + i][32 * quadrant : 32 * quadrant + 32, :], in_=src)
 
-        def load_row_values(b):
+        def load_row_values():
             given = (("sharp", sharp), ("share", share), ("least", least), ("gain", gain))
-            per_row = {}
-            if b == 0:
-                as_rows = keep.tile([P, P], F32, name="as_rows")
-                identity = keep.tile([P, P], F32, name="identity")
-                nc.gpsimd.memset(as_rows[:], 0.0)
-                make_identity(nc, identity[:])
-                for n, (name, ap) in enumerate(given):
-                    nc.sync.dma_start(out=as_rows[PACK * n : PACK * (n + 1), :], in_=ap[:PASS].rearrange("(t p) -> t p", p=P))
-                turned = psum.tile([P, P], F32, name="turned", tag="bank5")
-                nc.tensor.transpose(turned[:], as_rows[:], identity[:])
-                as_cols = keep.tile([P, len(given) * PACK], F32, name="as_cols")
-                nc.scalar.copy(out=as_cols[:], in_=turned[:, : len(given) * PACK])
-                for n, (name, ap) in enumerate(given):
-                    per_row[name] = as_cols[:, PACK * n : PACK * (n + 1)]
-            else:
-                for name, ap in given:
-                    loaded = keep.tile([P, PACK], F32, name=name)
-                    nc.sync.dma_start(out=loaded[:], in_=ap[PASS:].rearrange("(p i) -> p i", i=PACK))
-                    per_row[name] = loaded[:]
+            as_rows = keep.tile([P, H], F32, name="as_rows")
+            identity = keep.tile([P, P], F32, name="identity")
+            nc.gpsimd.memset(as_rows[:], 0.0)
+            make_identity(nc, identity[:])
+            for n, (name, ap) in enumerate(given):
+                nc.sync.dma_start(out=as_rows[n : n + 1, :], in_=ap.rearrange("(one r) -> one r", one=1))
+            as_cols = keep.tile([P, len(given), TILES], F32, name="as_cols")
+            for b in range(HP):
+                turned = psum.tile([P, PACK, P], F32, name="turned", tag="bank%d" % (4 + b))
+                for i in range(PACK):
+                    cols = slice(P * i, P * (i + 1)) if b == 0 else slice(PASS + i, H, PACK)
+                    nc.tensor.transpose(turned[:, i, :], as_rows[:, cols], identity[:])
+                nc.scalar.copy(
+                    out=as_cols[:, :, PACK * b : PACK * (b + 1)], in_=turned[:, :, : len(given)].rearrange("p i n -> p n i")
+                )
+            for n, (name, ap) in enumerate(given):
+                vec[name] = as_cols[:, n, :]
             for name in ("slope", "neg_least", "floor"):
-                derived = keep.tile([P, PACK], F32, name="%s%d" % (name, b))
-                per_row[name] = derived[:]
-            slope = per_row["slope"]
-            nc.gpsimd.tensor_tensor(out=slope, in0=per_row["sharp"], in1=per_row["share"], op=ALU.mult)
-            nc.gpsimd.tensor_scalar(out=slope, in0=slope, scalar1=-1.0, scalar2=0.0, op0=ALU.mult, op1=ALU.add)
-            nc.gpsimd.tensor_scalar(
-                out=per_row["neg_least"], in0=per_row["least"], scalar1=-1.0, scalar2=0.0, op0=ALU.mult, op1=ALU.add
-            )
-            nc.gpsimd.tensor_tensor(out=per_row["floor"], in0=per_row["gain"], in1=per_row["least"], op=ALU.mult)
-            vec[b] = per_row
+                derived = keep.tile([P, TILES], F32, name=name)
+                vec[name] = derived[:]
+            nc.gpsimd.tensor_tensor(out=vec["slope"], in0=vec["sharp"], in1=vec["share"], op=ALU.mult)
+            nc.gpsimd.tensor_scalar(out=vec["slope"], in0=vec["slope"], scalar1=-1.0, scalar2=0.0, op0=ALU.mult, op1=ALU.add)
+            nc.gpsimd.tensor_scalar(out=vec["neg_least"], in0=vec["least"], scalar1=-1.0, scalar2=0.0, op0=ALU.mult, op1=ALU.add)
+            nc.gpsimd.tensor_tensor(out=vec["floor"], in0=vec["gain"], in1=vec["least"], op=ALU.mult)
 
         def first_product(t):
             for c in range(2):
@@ -216,40 +215,43 @@ def tile_list_box_placement_balance_kernel(
                     )
 
         def new_scores(t):
-            rw = room_t[t]
             if t == 0:
                 for c in range(2):
                     h_t[0, c] = on_scores(0, 2 * S * c, [P, BANK], F32, "h0_%d" % c)
-                    nc.gpsimd.tensor_tensor(out=rw[:, halves[c]], in0=rw[:, halves[c]], in1=wgs_sb[:, halves[c]], op=ALU.mult)
-                    nc.vector.tensor_tensor(out=h_t[0, c][:], in0=acc1[t, c][:], in1=rw[:, halves[c]], op=ALU.mult)
+                    nc.vector.tensor_tensor(out=h_t[0, c][:], in0=acc1[t, c][:], in1=room_t[t][:, halves[c]], op=ALU.mult)
             else:
                 h_t[t] = on_scores(t, 0, [P, S], F32, "h%d" % t)
-                nc.gpsimd.tensor_tensor(out=rw[:], in0=rw[:], in1=wgs_t[t][:], op=ALU.mult)
                 for c in range(2):
                     h = h_t[t][:, halves[c]]
                     nc.scalar.copy(out=h, in_=acc1[t, c][:])
-                    nc.gpsimd.tensor_tensor(out=h, in0=h, in1=rw[:, halves[c]], op=ALU.mult)
+                    nc.gpsimd.tensor_tensor(out=h, in0=h, in1=room_t[t][:, halves[c]], op=ALU.mult)
 
         def scatter(t):
             if t == 0:
                 for c in range(2):
-                    nc.vector.tensor_copy(out=page_t[t][:].indirect(idx2[:, 32 * c : 32 * c + 32]), in_=h_t[0, c][:])
+                    window = page_t[t][:].indirect(idx2[:, 32 * c : 32 * c + 32])
+                    nc.vector.tensor_tensor(out=window, in0=h_t[0, c][:], in1=wgs_sb[:, halves[c]], op=ALU.mult)
             else:
-                nc.vector.tensor_copy(out=page_t[t][:].indirect(idx2[:]), in_=h_t[t][:])
+                nc.vector.tensor_tensor(out=page_t[t][:].indirect(idx2[:]), in0=h_t[t][:], in1=wgs_t[t][:], op=ALU.mult)
 
         def row_max(t):
             nc.vector.tensor_reduce(out=top[:, t : t + 1], in_=page_t[t][:], axis=AXIS.X, op=ALU.max)
 
         def look(t):
             b, i = divmod(t, PACK)
-            col = slice(i, i + 1)
-            per_row = vec[b]
-            nc.scalar.activation(out=bias[:, t : t + 1], in_=top[:, t : t + 1], func=ACT.Copy, scale=per_row["slope"][:, col])
-            x = work.tile([P, M], F32, name="x", tag="x")
+            col = slice(t, t + 1)
+            nc.scalar.activation(out=bias[:, t : t + 1], in_=top[:, t : t + 1], func=ACT.Copy, scale=vec["slope"][:, col])
+            x_t[t] = work.tile([P, M], F32, name="x", tag="x")
+            x = x_t[t]
             nc.scalar.activation(
                 out=x[:], in_=page_t[t][:].indirect(idx3[:]), func=ACT.Sigmoid,
-                bias=bias[:, t : t + 1], scale=per_row["sharp"][:, col],
+                bias=bias[:, t : t + 1], scale=vec["sharp"][:, col],
             )
+
+        def gate(t):
+            b, i = divmod(t, PACK)
+            col = slice(t, t + 1)
+            x = x_t[t]
             if b == 0:
                 y_plain[t] = keep.tile([P, M], BF16, name="y_plain%d" % t)
                 y = y_plain[t][:]
@@ -259,14 +261,14 @@ def tile_list_box_placement_balance_kernel(
                 y = y_bf[b][:, :, i]
             if t == TILES - 1:
                 nc.vector.tensor_scalar(
-                    out=y, in0=x[:], scalar1=per_row["least"][:, col], scalar2=per_row["gain"][:, col],
+                    out=y, in0=x[:], scalar1=vec["least"][:, col], scalar2=vec["gain"][:, col],
                     op0=ALU.max, op1=ALU.mult,
                 )
             else:
                 above = work.tile([P, M], F32, name="above", tag="above")
-                nc.scalar.activation(out=above[:], in_=x[:], func=ACT.Relu, bias=per_row["neg_least"][:, col])
+                nc.scalar.activation(out=above[:], in_=x[:], func=ACT.Relu, bias=vec["neg_least"][:, col])
                 nc.scalar.activation(
-                    out=y, in_=above[:], func=ACT.Identity, bias=per_row["floor"][:, col], scale=per_row["gain"][:, col]
+                    out=y, in_=above[:], func=ACT.Identity, bias=vec["floor"][:, col], scale=vec["gain"][:, col]
                 )
 
         def deal_y():
@@ -284,30 +286,20 @@ def tile_list_box_placement_balance_kernel(
                 out=y_c[b][:].bitcast(FP8X4), scales=y_s[b][:], in_=y_bf[b][:].rearrange("p m i -> p (m i)")
             )
 
-        def second_pass(n, b):
-            cols = slice(P * n, P * (n + 1))
-            piece = 2 * b + n // 3
-            cols3 = slice(P * (n % 3), P * (n % 3 + 1))
+        def second_pass(n, which, b):
             if b == 0:
-                for which in range(2):
-                    acc2[n, which] = psum.tile([P, M], F32, name="acc2", tag="bank%d" % ((2 * n + which) % 8))
+                acc2[n, which] = psum.tile([P, M], F32, name="acc2", tag="bank%d" % ((2 * n + which) % 8))
+            if which == 0:
+                words = w4_w[:, b, 2 * P * n : 2 * P * (n + 1)].bitcast(FP4X4)
+                plane = w4_s[:, b, P * n : P * (n + 1)]
+            else:
+                piece = 2 * b + n // 3
+                cols = slice(P * (n % 3), P * (n % 3 + 1))
+                words = w3_c[piece][:, cols].bitcast(FP8X4)
+                plane = w3_s[piece][:, cols]
             nc.tensor.matmul_mx(
-                out=acc2[n, 0][:],
-                lhsT=w4_w[:, b, 2 * P * n : 2 * P * (n + 1)].bitcast(FP4X4),
-                lhsT_scale=w4_s[:, b, cols],
-                rhs=y_c[b][:].bitcast(FP8X4),
-                rhs_scale=y_s[b][:],
-                start=(b == 0),
-                stop=(b == HP - 1),
-            )
-            nc.tensor.matmul_mx(
-                out=acc2[n, 1][:],
-                lhsT=w3_c[piece][:, cols3].bitcast(FP8X4),
-                lhsT_scale=w3_s[piece][:, cols3],
-                rhs=y_c[b][:].bitcast(FP8X4),
-                rhs_scale=y_s[b][:],
-                start=(b == 0),
-                stop=(b == HP - 1),
+                out=acc2[n, which][:], lhsT=words, lhsT_scale=plane, rhs=y_c[b][:].bitcast(FP8X4), rhs_scale=y_s[b][:],
+                start=(b == 0), stop=(b == HP - 1),
             )
 
         def finish(n):
@@ -325,31 +317,35 @@ def tile_list_box_placement_balance_kernel(
         nc.gpsimd.memset(w4_s[:].bitcast(I32), 0)
         nc.sync.dma_start(out=idx[:], in_=offs)
         load_tab(0, 4)
-        grouped0 = round_w1(0)
+        grouped0 = round_w1(0, load_w1(0))
         for q in range(4):
             nc.sync.dma_start(
                 out=tab_s[32 * q : 32 * q + 4 * KP, :].bitcast(I32), in_=tab_scales[:, 4 * q : 4 * q + 4, :].bitcast(I32)
             )
         load_tab(1, 1)
+        load_row_values()
         load_tab(2, 1)
         nc.vector.tensor_copy(out=v_s[:], in_=tab_s[:].indirect(idx[:]))
         quant_w1(0, grouped0)
         for a in range(KP):
             for c in range(2):
                 gather_words(a, c)
-        room_t[0] = stage.tile([P, S], F32, name="room", tag="room")
+        room_t[0] = stage.tile([P, S], F32, name="room", tag="room", bufs=2)
         load_room(0, halves[0])
         nc.sync.dma_start(out=wgs_sb[:, halves[0]], in_=wgs[:, halves[0]])
         nc.sync.dma_start(out=idx2[:], in_=offs2)
         load_page(0)
-        grouped1 = round_w1(1)
+        grouped1 = round_w1(1, load_w1(1))
         load_room(0, halves[1])
         nc.sync.dma_start(out=wgs_sb[:, halves[1]], in_=wgs[:, halves[1]])
         first_product(0)
         new_scores(0)
 
         def next_room(t):
-            room_t[t] = stage.tile([P, S], F32, name="room", tag="room")
+            if t < PACK:
+                room_t[t] = stage.tile([P, S], F32, name="room", tag="room", bufs=2)
+            else:
+                room_t[t] = stage.tile([P, S], F32, name="late_room", tag="late_room", bufs=1)
             load_room(t, whole)
 
         def next_scores(t):
@@ -359,16 +355,17 @@ def tile_list_box_placement_balance_kernel(
         scatter(0)
         quant_w1(1, grouped1)
         next_room(1)
-        grouped2 = round_w1(2)
+        raw2 = load_w1(2)
         nc.sync.dma_start(out=idx3[:], in_=offs3)
-        load_row_values(0)
         load_page(1)
         next_scores(1)
+        grouped2 = round_w1(2, raw2)
         row_max(0)
         quant_w1(2, grouped2)
         look(0)
+        gate(0)
 
-        grouped3 = round_w1(3)
+        grouped3 = round_w1(3, load_w1(3))
         scatter(1)
         next_room(2)
         raw_wide = [load_w1_wide(0), load_w1_wide(1)]
@@ -378,19 +375,21 @@ def tile_list_box_placement_balance_kernel(
         row_max(1)
         quant_w1(3, grouped3)
         look(1)
+        gate(1)
 
-        wide.append(round_w1_wide(load_w1_wide(2)))
+        raw_last = load_w1_wide(2)
         scatter(2)
         next_room(3)
         load_wgs_dealt(0)
         load_page(3)
         next_scores(3)
+        wide.append(round_w1_wide(raw_last))
         row_max(2)
         quant_w1_wide(0, 2, 0, wide[0])
         quant_w1_wide(1, 2, 2 * S, wide[1])
         quant_w1_wide(2, 1, 0, wide[2])
         look(2)
-        load_row_values(1)
+        gate(2)
 
         waiting = []
         for t in range(KP, TILES):
@@ -423,12 +422,15 @@ def tile_list_box_placement_balance_kernel(
             if t == TILES - 1:
                 quant_y(0)
                 for n in range(4):
-                    second_pass(n, 0)
+                    for which in range(2):
+                        second_pass(n, which, 0)
             look(t)
+            gate(t)
 
         quant_y(1)
         for n in range(NT):
-            if n >= 4:
-                second_pass(n, 0)
-            second_pass(n, 1)
+            for which in range(2):
+                if n >= 4:
+                    second_pass(n, which, 0)
+                second_pass(n, which, 1)
             finish(n)

@@ -57,7 +57,7 @@ def tile_list_box_placement_balance_kernel(
         y_bf = {}
         w4_w = keep.tile([P, HP, 2 * N], U8, name="w4_w", align_bytes=64)
         w4_s = keep.tile([P, HP, N], U8, name="w4_s", align_bytes=64)
-        top = keep.tile([P, TILES], F32, name="top")
+        top = {}
         bias = keep.tile([P, TILES], F32, name="bias")
         w1_c = {}
         w1_s = {}
@@ -141,11 +141,14 @@ def tile_list_box_placement_balance_kernel(
             for i in range(PACK):
                 lhs[PACK + i, a] = (codes[:, P * i : P * (i + 1)], planes[:, P * i : P * (i + 1)])
 
-        def round_w3(piece):
+        def load_w3(piece):
             b, c = divmod(piece, 2)
-            raw = stage.tile([P, PACK, W3_PIECE], F32, name="raw3", tag="raw3", bufs=2)
+            raw = stage.tile([P, PACK, W3_PIECE], F32, name="raw3", tag="raw", bufs=4)
             src = w3[PASS * b : PASS * (b + 1), W3_PIECE * c : W3_PIECE * (c + 1)]
             nc.sync.dma_start(out=raw[:], in_=src.rearrange("(p j) c -> p j c", j=PACK))
+            return raw
+
+        def round_w3(raw):
             grouped = stage.tile([P, PACK * W3_PIECE], BF16, name="grouped3", tag="grouped3", align_bytes=64)
             nc.scalar.copy(*interleaved(grouped[:], raw[:]))
             return grouped
@@ -222,9 +225,10 @@ def tile_list_box_placement_balance_kernel(
             else:
                 h_t[t] = on_scores(t, 0, [P, S], F32, "h%d" % t)
                 for c in range(2):
-                    h = h_t[t][:, halves[c]]
-                    nc.scalar.copy(out=h, in_=acc1[t, c][:])
-                    nc.gpsimd.tensor_tensor(out=h, in0=h, in1=room_t[t][:, halves[c]], op=ALU.mult)
+                    nc.scalar.copy(out=h_t[t][:, halves[c]], in_=acc1[t, c][:])
+                for cols in halves if t <= PACK else [whole]:
+                    h = h_t[t][:, cols]
+                    nc.gpsimd.tensor_tensor(out=h, in0=h, in1=room_t[t][:, cols], op=ALU.mult)
 
         def scatter(t):
             if t == 0:
@@ -235,12 +239,16 @@ def tile_list_box_placement_balance_kernel(
                 nc.vector.tensor_tensor(out=page_t[t][:].indirect(idx2[:]), in0=h_t[t][:], in1=wgs_t[t][:], op=ALU.mult)
 
         def row_max(t):
-            nc.vector.tensor_reduce(out=top[:, t : t + 1], in_=page_t[t][:], axis=AXIS.X, op=ALU.max)
+            if KP <= t < TILES - 2:
+                top[t] = on_scores(t + 2, 0, [P, 1], F32, "top%d" % t)
+            else:
+                top[t] = keep.tile([P, 1], F32, name="top%d" % t)
+            nc.vector.tensor_reduce(out=top[t][:], in_=page_t[t][:], axis=AXIS.X, op=ALU.max)
 
         def look(t):
             b, i = divmod(t, PACK)
             col = slice(t, t + 1)
-            nc.scalar.activation(out=bias[:, t : t + 1], in_=top[:, t : t + 1], func=ACT.Copy, scale=vec["slope"][:, col])
+            nc.scalar.activation(out=bias[:, t : t + 1], in_=top[t][:], func=ACT.Copy, scale=vec["slope"][:, col])
             x_t[t] = work.tile([P, M], F32, name="x", tag="x")
             x = x_t[t]
             nc.scalar.activation(
@@ -330,22 +338,19 @@ def tile_list_box_placement_balance_kernel(
         for a in range(KP):
             for c in range(2):
                 gather_words(a, c)
-        room_t[0] = stage.tile([P, S], F32, name="room", tag="room", bufs=2)
+        room_t[0] = stage.tile([P, S], F32, name="room", tag="room")
         load_room(0, halves[0])
         nc.sync.dma_start(out=wgs_sb[:, halves[0]], in_=wgs[:, halves[0]])
         nc.sync.dma_start(out=idx2[:], in_=offs2)
         load_page(0)
         grouped1 = round_w1(1, load_w1(1))
-        load_room(0, halves[1])
         nc.sync.dma_start(out=wgs_sb[:, halves[1]], in_=wgs[:, halves[1]])
+        load_room(0, halves[1])
         first_product(0)
         new_scores(0)
 
         def next_room(t):
-            if t < PACK:
-                room_t[t] = stage.tile([P, S], F32, name="room", tag="room", bufs=2)
-            else:
-                room_t[t] = stage.tile([P, S], F32, name="late_room", tag="late_room", bufs=1)
+            room_t[t] = stage.tile([P, S], F32, name="room", tag="room")
             load_room(t, whole)
 
         def next_scores(t):
@@ -391,23 +396,24 @@ def tile_list_box_placement_balance_kernel(
         look(2)
         gate(2)
 
-        waiting = []
+        loaded = []
         for t in range(KP, TILES):
             scatter(t)
-            ready = waiting
-            waiting = []
             if t + 1 < TILES:
                 next_room(t + 1)
                 load_page(t + 1)
                 next_scores(t + 1)
+            rounded = [(piece, round_w3(raw)) for piece, raw in loaded]
+            if t > KP:
+                gate(t - 1)
+            loaded = []
             if t + 2 < TILES:
-                pieces = ([0], [1, 2], [3])[t - KP]
-                waiting = [(piece, round_w3(piece)) for piece in pieces]
+                loaded = [(piece, load_w3(piece)) for piece in ([0, 1], [2], [3])[t - KP]]
                 load_wgs_dealt(t + 2 - PACK)
             if t == TILES - 3:
                 deal_y()
             row_max(t)
-            for n, (piece, grouped) in enumerate(ready):
+            for n, (piece, grouped) in enumerate(rounded):
                 quant_w3(piece, t, 2 * S * n, grouped)
             if t == TILES - 2:
                 nc.sync.dma_start(out=w4_w[:].bitcast(I32), in_=w4_words.rearrange("b p c -> p b c").bitcast(I32))
@@ -425,8 +431,8 @@ def tile_list_box_placement_balance_kernel(
                     for which in range(2):
                         second_pass(n, which, 0)
             look(t)
-            gate(t)
 
+        gate(TILES - 1)
         quant_y(1)
         for n in range(NT):
             for which in range(2):

from contextlib import ExitStack

import concourse.mybir as mybir
from concourse.masks import make_identity

K, H, N, T, S, T2, M = 1536, 1024, 768, 2048, 1024, 2048, 512
FLOPS = 2 * K * H * S + 2 * 2 * H * N * M

F32 = mybir.dt.float32
BF16 = mybir.dt.bfloat16
I32 = mybir.dt.int32
U32 = mybir.dt.uint32
U16 = mybir.dt.uint16
U8 = mybir.dt.uint8
FP8X4 = mybir.dt.float8_e4m3fn_x4
FP4X4 = mybir.dt.float4_e2m1fn_x4
ACT = mybir.ActivationFunctionType
ALU = mybir.AluOpType
AXIS = mybir.AxisListType

P = 128
PACK = 4
PASS = P * PACK
BANK = 512
KP = K // PASS
HP = H // PASS
TILES = H // P
NT = N // P
W3_PIECE = 384


def tile_list_box_placement_balance_kernel(
    tc, tab_words, tab_scales, offs, offs2, offs3, w1, room, wgs, page0,
    sharp, share, least, gain, w4_words, w4_scales, w3, bal, out,
):
    nc = tc.nc
    with ExitStack() as ctx:
        lists = ctx.enter_context(tc.tile_pool(name="lists", bufs=1))
        keep = ctx.enter_context(tc.tile_pool(name="keep", bufs=1))
        stage = ctx.enter_context(tc.tile_pool(name="stage", bufs=3))
        pages = ctx.enter_context(tc.tile_pool(name="pages", bufs=4))
        work = ctx.enter_context(tc.tile_pool(name="work", bufs=2))
        scores = ctx.enter_context(tc.tile_pool(name="scores", bufs=1))
        table = ctx.enter_context(tc.tile_pool(name="table", bufs=1))
        psum = ctx.enter_context(tc.psum_pool(name="psum", bufs=1))

        idx = lists.tile([P, S // 16], U16, name="idx")
        idx2 = lists.tile([P, S // 16], U16, name="idx2")
        idx3 = lists.tile([P, M // 16], U16, name="idx3")

        tab_w = [table.tile([P, T], I32, name="tab_w%d" % a, offset=4 * T * a) for a in range(KP)]
        tab_s = keep.tile([P, T], U8, name="tab_s")
        v_w = [[keep.tile([P, BANK], U32, name="v_w%d_%d" % (a, c), align_bytes=64) for c in range(2)] for a in range(KP)]
        v_s = keep.tile([P, S], U8, name="v_s", align_bytes=64)
        wgs_sb = keep.tile([P, S], F32, name="wgs_sb")
        wgs_t = {t: wgs_sb for t in range(PACK)}
        y_bf = {}
        w4_w = keep.tile([P, HP, 2 * N], U8, name="w4_w", align_bytes=64)
        w4_s = keep.tile([P, HP, N], U8, name="w4_s", align_bytes=64)
        top = {}
        bias = keep.tile([P, TILES], F32, name="bias")
        w1_c = {}
        w1_s = {}
        lhs = {}
        w3_c = {}
        w3_s = {}
        y_plain = {}
        y_c = {}
        y_s = {}
        room_t = {}
        page_t = {}
        h_t = {}
        x_t = {}
        acc1 = {}
        acc2 = {}
        bal_t = {}
        vec = {}
        halves = [slice(BANK * c, BANK * (c + 1)) for c in range(2)]
        whole = slice(0, S)

        def on_scores(t, at, shape, dtype, name):
            return scores.tile(shape, dtype, name=name, offset=4 * S * t + at, align_bytes=64)

        def load_tab(a, pieces):
            src = tab_words[a].rearrange("p t i -> p (t i)").bitcast(I32)
            for c0 in range(0, T, T // pieces):
                cols = slice(c0, c0 + T // pieces)
                nc.sync.dma_start(out=tab_w[a][:, cols], in_=src[:, cols])

        def gather_words(a, c):
            nc.vector.tensor_copy(out=v_w[a][c][:], in_=tab_w[a][:].bitcast(U32).indirect(idx[:, 32 * c : 32 * c + 32]))

        def interleaved(out, in_):
            return (
                out.rearrange("p (c e j) -> p c j e", e=PACK, j=PACK),
                in_.rearrange("p j (c e) -> p c j e", e=PACK),
            )

        def load_w1(t):
            raw = stage.tile([P, KP, PACK, P], F32, name="raw1", tag="raw", bufs=4)
            for a in range(KP):
                src = w1[PASS * a : PASS * (a + 1), P * t : P * (t + 1)]
                nc.sync.dma_start(out=raw[:, a, :, :], in_=src.rearrange("(p j) c -> p j c", j=PACK))
            return raw

        def round_w1(t, raw):
            grouped = stage.tile([P, KP * PASS], BF16, name="grouped1", tag="grouped", align_bytes=64)
            for a in range(KP):
                nc.scalar.copy(*interleaved(grouped[:, PASS * a : PASS * (a + 1)], raw[:, a, :, :]))
            return grouped

        def quant_w1(t, grouped):
            if t == 0:
                w1_c[t] = keep.tile([P, KP * P], U32, name="w1_c0", align_bytes=64)
            elif t == 1:
                w1_c[t] = on_scores(0, 0, [P, KP * P], U32, "w1_c1")
            else:
                w1_c[t] = on_scores(t - 2, 2 * S, [P, KP * P], U32, "w1_c%d" % t)
            w1_s[t] = keep.tile([P, KP * P], U8, name="w1_s%d" % t, align_bytes=64)
            nc.vector.quantize_mx(out=w1_c[t][:].bitcast(FP8X4), scales=w1_s[t][:], in_=grouped[:])
            for a in range(KP):
                lhs[t, a] = (w1_c[t][:, P * a : P * (a + 1)], w1_s[t][:, P * a : P * (a + 1)])

        def load_w1_wide(a):
            raw = stage.tile([P, PACK, PASS], F32, name="raw2", tag="raw", bufs=4)
            nc.sync.dma_start(out=raw[:], in_=w1[PASS * a : PASS * (a + 1), PASS:].rearrange("(p j) c -> p j c", j=PACK))
            return raw

        def round_w1_wide(raw):
            grouped = stage.tile([P, PACK * PASS], BF16, name="grouped2", tag="grouped", align_bytes=64)
            nc.scalar.copy(
                out=grouped[:].rearrange("p (i q j) -> p q i j", i=PACK, j=PACK),
                in_=raw[:].rearrange("p j (q i) -> p q i j", i=PACK),
            )
            return grouped

        def quant_w1_wide(a, host, at, grouped):
            codes = on_scores(host, at, [P, PASS], U32, "w1w_c%d" % a)
            planes = keep.tile([P, PASS], U8, name="w1w_s%d" % a, align_bytes=64)
            nc.vector.quantize_mx(out=codes[:].bitcast(FP8X4), scales=planes[:], in_=grouped[:])
            for i in range(PACK):
                lhs[PACK + i, a] = (codes[:, P * i : P * (i + 1)], planes[:, P * i : P * (i + 1)])

        def load_w3(piece):
            b, c = divmod(piece, 2)
            raw = stage.tile([P, PACK, W3_PIECE], F32, name="raw3", tag="raw", bufs=4)
            src = w3[PASS * b : PASS * (b + 1), W3_PIECE * c : W3_PIECE * (c + 1)]
            nc.sync.dma_start(out=raw[:], in_=src.rearrange("(p j) c -> p j c", j=PACK))
            return raw

        def round_w3(raw):
            grouped = stage.tile([P, PACK * W3_PIECE], BF16, name="grouped3", tag="grouped3", align_bytes=64)
            nc.scalar.copy(*interleaved(grouped[:], raw[:]))
            return grouped

        def quant_w3(piece, host, at, grouped):
            w3_c[piece] = on_scores(host, at, [P, W3_PIECE], U32, "w3_c%d" % piece)
            w3_s[piece] = keep.tile([P, W3_PIECE], U8, name="w3_s%d" % piece, align_bytes=64)
            nc.vector.quantize_mx(out=w3_c[piece][:].bitcast(FP8X4), scales=w3_s[piece][:], in_=grouped[:])

        def rows(ap, t):
            if t < PACK:
                return ap[P * t : P * (t + 1), :]
            return ap[PASS:, :].rearrange("(p i) c -> i p c", i=PACK)[t - PACK]

        def load_room(t, cols):
            nc.sync.dma_start(out=room_t[t][:, cols], in_=rows(room, t)[:, cols])

        def load_page(t):
            page_t[t] = pages.tile([P, T2], F32, name="page", tag="page")
            nc.sync.dma_start(out=page_t[t][:], in_=rows(page0, t))

        def load_wgs_dealt(i):
            wgs_t[PACK + i] = table.tile([P, S], F32, name="wgs%d" % i, offset=4 * S * i)
            src = wgs.rearrange("(q i) j -> i q j", i=PACK)[i]
            for quadrant in (0, 2, 1, 3):
                nc.sync.dma_start(out=wgs_t[PACK + i][32 * quadrant : 32 * quadrant + 32, :], in_=src)

        def load_row_values():
            given = (("sharp", sharp), ("share", share), ("least", least), ("gain", gain))
            as_rows = keep.tile([P, H], F32, name="as_rows")
            identity = keep.tile([P, P], F32, name="identity")
            nc.gpsimd.memset(as_rows[:], 0.0)
            make_identity(nc, identity[:])
            for n, (name, ap) in enumerate(given):
                nc.sync.dma_start(out=as_rows[n : n + 1, :], in_=ap.rearrange("(one r) -> one r", one=1))
            as_cols = keep.tile([P, len(given), TILES], F32, name="as_cols")
            for b in range(HP):
                turned = psum.tile([P, PACK, P], F32, name="turned", tag="bank%d" % (4 + b))
                for i in range(PACK):
                    cols = slice(P * i, P * (i + 1)) if b == 0 else slice(PASS + i, H, PACK)
                    nc.tensor.transpose(turned[:, i, :], as_rows[:, cols], identity[:])
                nc.scalar.copy(
                    out=as_cols[:, :, PACK * b : PACK * (b + 1)], in_=turned[:, :, : len(given)].rearrange("p i n -> p n i")
                )
            for n, (name, ap) in enumerate(given):
                vec[name] = as_cols[:, n, :]
            for name in ("slope", "neg_least", "floor"):
                derived = keep.tile([P, TILES], F32, name=name)
                vec[name] = derived[:]
            nc.gpsimd.tensor_tensor(out=vec["slope"], in0=vec["sharp"], in1=vec["share"], op=ALU.mult)
            nc.gpsimd.tensor_scalar(out=vec["slope"], in0=vec["slope"], scalar1=-1.0, scalar2=0.0, op0=ALU.mult, op1=ALU.add)
            nc.gpsimd.tensor_scalar(out=vec["neg_least"], in0=vec["least"], scalar1=-1.0, scalar2=0.0, op0=ALU.mult, op1=ALU.add)
            nc.gpsimd.tensor_tensor(out=vec["floor"], in0=vec["gain"], in1=vec["least"], op=ALU.mult)

        def first_product(t):
            for c in range(2):
                acc1[t, c] = psum.tile([P, BANK], F32, name="acc1", tag="bank%d" % (2 * (t % 2) + c))
                for a in range(KP):
                    nc.tensor.matmul_mx(
                        out=acc1[t, c][:],
                        lhsT=lhs[t, a][0].bitcast(FP8X4),
                        lhsT_scale=lhs[t, a][1],
                        rhs=v_w[a][c][:].bitcast(FP8X4),
                        rhs_scale=v_s[4 * a : P, halves[c]],
                        start=(a == 0),
                        stop=(a == KP - 1),
                    )

        def new_scores(t):
            if t == 0:
                for c in range(2):
                    h_t[0, c] = on_scores(0, 2 * S * c, [P, BANK], F32, "h0_%d" % c)
                    nc.vector.tensor_tensor(out=h_t[0, c][:], in0=acc1[t, c][:], in1=room_t[t][:, halves[c]], op=ALU.mult)
            else:
                h_t[t] = on_scores(t, 0, [P, S], F32, "h%d" % t)
                for c in range(2):
                    nc.scalar.copy(out=h_t[t][:, halves[c]], in_=acc1[t, c][:])
                for cols in halves if t <= PACK else [whole]:
                    h = h_t[t][:, cols]
                    nc.gpsimd.tensor_tensor(out=h, in0=h, in1=room_t[t][:, cols], op=ALU.mult)

        def scatter(t):
            if t == 0:
                for c in range(2):
                    window = page_t[t][:].indirect(idx2[:, 32 * c : 32 * c + 32])
                    nc.vector.tensor_tensor(out=window, in0=h_t[0, c][:], in1=wgs_sb[:, halves[c]], op=ALU.mult)
            else:
                nc.vector.tensor_tensor(out=page_t[t][:].indirect(idx2[:]), in0=h_t[t][:], in1=wgs_t[t][:], op=ALU.mult)

        def row_max(t):
            if KP <= t < TILES - 2:
                top[t] = on_scores(t + 2, 0, [P, 1], F32, "top%d" % t)
            else:
                top[t] = keep.tile([P, 1], F32, name="top%d" % t)
            nc.vector.tensor_reduce(out=top[t][:], in_=page_t[t][:], axis=AXIS.X, op=ALU.max)

        def look(t):
            b, i = divmod(t, PACK)
            col = slice(t, t + 1)
            nc.scalar.activation(out=bias[:, t : t + 1], in_=top[t][:], func=ACT.Copy, scale=vec["slope"][:, col])
            x_t[t] = work.tile([P, M], F32, name="x", tag="x")
            x = x_t[t]
            nc.scalar.activation(
                out=x[:], in_=page_t[t][:].indirect(idx3[:]), func=ACT.Sigmoid,
                bias=bias[:, t : t + 1], scale=vec["sharp"][:, col],
            )

        def gate(t):
            b, i = divmod(t, PACK)
            col = slice(t, t + 1)
            x = x_t[t]
            if b == 0:
                y_plain[t] = keep.tile([P, M], BF16, name="y_plain%d" % t)
                y = y_plain[t][:]
            else:
                if i == 0:
                    y_bf[b] = keep.tile([P, M, PACK], BF16, name="y_bf1", align_bytes=64)
                y = y_bf[b][:, :, i]
            if t == TILES - 1:
                nc.vector.tensor_scalar(
                    out=y, in0=x[:], scalar1=vec["least"][:, col], scalar2=vec["gain"][:, col],
                    op0=ALU.max, op1=ALU.mult,
                )
            else:
                above = work.tile([P, M], F32, name="above", tag="above")
                nc.scalar.activation(out=above[:], in_=x[:], func=ACT.Relu, bias=vec["neg_least"][:, col])
                nc.scalar.activation(
                    out=y, in_=above[:], func=ACT.Identity, bias=vec["floor"][:, col], scale=vec["gain"][:, col]
                )

        def deal_y():
            dealt = table.tile([P, PACK, M], BF16, name="y_dealt", offset=4 * S * PACK)
            for t in range(PACK):
                for i in range(PACK):
                    nc.sync.dma_start(out=dealt[32 * t : 32 * t + 32, i, :], in_=y_plain[t][i:P:PACK, :])
            y_bf[0] = keep.tile([P, M, PACK], BF16, name="y_bf0", align_bytes=64)
            nc.scalar.copy(*interleaved(y_bf[0][:].rearrange("p m i -> p (m i)"), dealt[:]))

        def quant_y(b):
            y_c[b] = on_scores(TILES - 1, 4 * M * b, [P, M], U32, "y_c%d" % b)
            y_s[b] = keep.tile([P, M], U8, name="y_s%d" % b, align_bytes=64)
            nc.vector.quantize_mx(
                out=y_c[b][:].bitcast(FP8X4), scales=y_s[b][:], in_=y_bf[b][:].rearrange("p m i -> p (m i)")
            )

        def second_pass(n, which, b):
            if b == 0:
                acc2[n, which] = psum.tile([P, M], F32, name="acc2", tag="bank%d" % ((2 * n + which) % 8))
            if which == 0:
                words = w4_w[:, b, 2 * P * n : 2 * P * (n + 1)].bitcast(FP4X4)
                plane = w4_s[:, b, P * n : P * (n + 1)]
            else:
                piece = 2 * b + n // 3
                cols = slice(P * (n % 3), P * (n % 3 + 1))
                words = w3_c[piece][:, cols].bitcast(FP8X4)
                plane = w3_s[piece][:, cols]
            nc.tensor.matmul_mx(
                out=acc2[n, which][:], lhsT=words, lhsT_scale=plane, rhs=y_c[b][:].bitcast(FP8X4), rhs_scale=y_s[b][:],
                start=(b == 0), stop=(b == HP - 1),
            )

        def finish(n):
            res = bal_t[n]
            nc.vector.tensor_tensor(out=res[:], in0=acc2[n, 0][:], in1=res[:], op=ALU.mult)
            if n < 4:
                other = work.tile([P, M], F32, name="other", tag="other")
                nc.scalar.copy(out=other[:], in_=acc2[n, 1][:])
                nc.gpsimd.tensor_tensor(out=res[:], in0=res[:], in1=other[:], op=ALU.add)
            else:
                nc.vector.tensor_tensor(out=res[:], in0=acc2[n, 1][:], in1=res[:], op=ALU.add)
            nc.sync.dma_start(out=out[P * n : P * (n + 1), :], in_=res[:])

        nc.gpsimd.memset(tab_s[:].bitcast(I32), 0)
        nc.gpsimd.memset(w4_s[:].bitcast(I32), 0)
        nc.sync.dma_start(out=idx[:], in_=offs)
        load_tab(0, 4)
        grouped0 = round_w1(0, load_w1(0))
        for q in range(4):
            nc.sync.dma_start(
                out=tab_s[32 * q : 32 * q + 4 * KP, :].bitcast(I32), in_=tab_scales[:, 4 * q : 4 * q + 4, :].bitcast(I32)
            )
        load_tab(1, 1)
        load_row_values()
        load_tab(2, 1)
        nc.vector.tensor_copy(out=v_s[:], in_=tab_s[:].indirect(idx[:]))
        quant_w1(0, grouped0)
        for a in range(KP):
            for c in range(2):
                gather_words(a, c)
        room_t[0] = stage.tile([P, S], F32, name="room", tag="room")
        load_room(0, halves[0])
        nc.sync.dma_start(out=wgs_sb[:, halves[0]], in_=wgs[:, halves[0]])
        nc.sync.dma_start(out=idx2[:], in_=offs2)
        load_page(0)
        grouped1 = round_w1(1, load_w1(1))
        nc.sync.dma_start(out=wgs_sb[:, halves[1]], in_=wgs[:, halves[1]])
        load_room(0, halves[1])
        first_product(0)
        new_scores(0)

        def next_room(t):
            room_t[t] = stage.tile([P, S], F32, name="room", tag="room")
            load_room(t, whole)

        def next_scores(t):
            first_product(t)
            new_scores(t)

        scatter(0)
        quant_w1(1, grouped1)
        next_room(1)
        raw2 = load_w1(2)
        nc.sync.dma_start(out=idx3[:], in_=offs3)
        load_page(1)
        next_scores(1)
        grouped2 = round_w1(2, raw2)
        row_max(0)
        quant_w1(2, grouped2)
        look(0)
        gate(0)

        grouped3 = round_w1(3, load_w1(3))
        scatter(1)
        next_room(2)
        raw_wide = [load_w1_wide(0), load_w1_wide(1)]
        load_page(2)
        next_scores(2)
        wide = [round_w1_wide(raw) for raw in raw_wide]
        row_max(1)
        quant_w1(3, grouped3)
        look(1)
        gate(1)

        raw_last = load_w1_wide(2)
        scatter(2)
        next_room(3)
        load_wgs_dealt(0)
        load_page(3)
        next_scores(3)
        wide.append(round_w1_wide(raw_last))
        row_max(2)
        quant_w1_wide(0, 2, 0, wide[0])
        quant_w1_wide(1, 2, 2 * S, wide[1])
        quant_w1_wide(2, 1, 0, wide[2])
        look(2)
        gate(2)

        loaded = []
        for t in range(KP, TILES):
            scatter(t)
            if t + 1 < TILES:
                next_room(t + 1)
                load_page(t + 1)
                next_scores(t + 1)
            rounded = [(piece, round_w3(raw)) for piece, raw in loaded]
            if t > KP:
                gate(t - 1)
            loaded = []
            if t + 2 < TILES:
                loaded = [(piece, load_w3(piece)) for piece in ([0, 1], [2], [3])[t - KP]]
                load_wgs_dealt(t + 2 - PACK)
            if t == TILES - 3:
                deal_y()
            row_max(t)
            for n, (piece, grouped) in enumerate(rounded):
                quant_w3(piece, t, 2 * S * n, grouped)
            if t == TILES - 2:
                nc.sync.dma_start(out=w4_w[:].bitcast(I32), in_=w4_words.rearrange("b p c -> p b c").bitcast(I32))
                for q in range(4):
                    nc.sync.dma_start(
                        out=w4_s[32 * q : 32 * q + 4, :, :].bitcast(I32),
                        in_=w4_scales[:, 4 * q : 4 * q + 4, :].rearrange("b r c -> r b c").bitcast(I32),
                    )
                for n in range(NT):
                    bal_t[n] = keep.tile([P, M], F32, name="bal%d" % n)
                    nc.sync.dma_start(out=bal_t[n][:], in_=bal[P * n : P * (n + 1), :])
            if t == TILES - 1:
                quant_y(0)
                for n in range(4):
                    for which in range(2):
                        second_pass(n, which, 0)
            look(t)

        gate(TILES - 1)
        quant_y(1)
        for n in range(NT):
            for which in range(2):
                if n >= 4:
                    second_pass(n, which, 0)
                second_pass(n, which, 1)
            finish(n)
